import numpy as np
import ml_dtypes


def mxq(x, axis, fmt="e4m3"):
    dtype, down = {"e4m3": (ml_dtypes.float8_e4m3fn, 7), "e5m2": (ml_dtypes.float8_e5m2, 14)}[fmt]
    v = np.moveaxis(np.asarray(x, np.float32).astype(ml_dtypes.bfloat16).astype(np.float64), axis, -1)
    blocks = v.reshape(v.shape[:-1] + (-1, 32))
    amax = np.abs(blocks).max(-1, keepdims=True)
    byte = np.maximum(np.where(amax > 0, np.frexp(amax)[1] - 1 + 127, 0) - down, 1)
    scale = np.exp2(byte - 127.0)
    codes = (blocks / scale).astype(np.float32).astype(dtype).astype(np.float64)
    return np.moveaxis((codes * scale).reshape(v.shape), -1, axis)


WIDE = False


def mx_kscale(k):
    if not WIDE:
        return np.ones(k)
    levels = np.array([10, -10, 5, -5, 0])
    if k % 512:
        return np.exp2(np.random.permutation(np.resize(levels, k // 32))).repeat(32)
    a = np.empty((k // 512, 16))
    for p in range(k // 512):
        a[p, :8] = np.random.permutation(np.resize(levels, 8))
        for g in range(8):
            far = levels[np.abs(levels - a[p, g]) >= 10]
            a[p, g + 8] = far[np.random.randint(len(far))]
    return np.exp2(a.ravel()).repeat(32)


def f64(x):
    return np.asarray(x).astype(np.float64)


def striped(idx):
    return np.tile(idx.reshape(-1, 16).T, (8, 1)).astype(np.uint16)


def unstriped(offs):
    return offs[:16].T.reshape(-1).astype(np.int64)


E2M1 = np.array([0.0, 0.5, 1.0, 1.5, 2.0, 3.0, 4.0, 6.0, -0.0, -0.5, -1.0, -1.5, -2.0, -3.0, -4.0, -6.0])


def pack_weight(w, fmt):
    k, n = w.shape
    w = f64(np.asarray(w, np.float32).astype(ml_dtypes.bfloat16)).reshape(k // 32, 32, n)
    amax = np.abs(w).max(1)
    if fmt == "e4m3":
        byte = np.frexp(amax)[1] - 1 + 127 - 7
    else:
        mant, ex = np.frexp(amax / 6.0)
        byte = np.where(mant > 0.5, ex, ex - 1) + 127
    byte = np.clip(np.where(amax > 0, byte, 1), 1, 254)
    scaled = (w * np.exp2(127.0 - byte)[:, None, :]).reshape(k, n).astype(np.float32)
    by_word = np.ascontiguousarray(scaled.reshape(k // 512, 128, 4, n).transpose(0, 1, 3, 2))
    if fmt == "e4m3":
        words = by_word.astype(ml_dtypes.float8_e4m3fn).view(np.uint8)
    else:
        c = by_word.astype(ml_dtypes.float4_e2m1fn).view(np.uint8) & 0xF
        words = (c[..., 0::2] | (c[..., 1::2] << 4)).reshape(k // 512, 128, 2 * n)
    return np.ascontiguousarray(words), np.ascontiguousarray(byte.astype(np.uint8).reshape(k // 512, 16, n))


def unpack_weight(words, scales, fmt):
    g, _, n = scales.shape
    words = np.ascontiguousarray(words).reshape(g, 128, n, -1)
    if fmt == "e4m3":
        vals = words.view(ml_dtypes.float8_e4m3fn).astype(np.float64)
    else:
        nib = np.empty((g, 128, n, 4), np.uint8)
        nib[..., 0::2] = words & 0xF
        nib[..., 1::2] = words >> 4
        vals = E2M1[nib]
    vals = vals * np.repeat(np.exp2(scales.astype(np.float64) - 127.0), 8, axis=1)[..., None]
    return vals.transpose(0, 1, 3, 2).reshape(g * 512, n)


def gelu(v):
    return 0.5 * v * (1.0 + np.tanh(np.sqrt(2.0 / np.pi) * (v + 0.044715 * v**3)))


def bf(x):
    return np.asarray(x, np.float32).astype(ml_dtypes.bfloat16)


def planes(Y):
    n, m = Y.shape
    b = f64(bf(Y)).reshape(n // 32, 32, m)
    amax = np.abs(b).max(1)
    byte = np.clip(np.where(amax > 0, np.frexp(amax)[1] - 1 + 127 - 7, 1), 1, 254)
    codes = (b * np.exp2(127.0 - byte)[:, None, :]).reshape(n, m).astype(np.float32).astype(ml_dtypes.float8_e4m3fn).view(np.uint8)
    words = codes.reshape(n // 512, 128, 4, m).transpose(0, 1, 3, 2)
    return np.ascontiguousarray(words), np.ascontiguousarray(byte.astype(np.uint8).reshape(n // 512, 16, m))


K, T, S, H, N = 1024, 2048, 1024, 512, 384

def setup_inputs():
    n = np.random.standard_normal
    s = mx_kscale(K)[:, None]
    u = mx_kscale(H)[:, None]
    tab_words, tab_scales = pack_weight(n((K, T)) * s, "e4m3")
    w2_words, w2_scales = pack_weight(n((K, H)) / np.sqrt(K) / s, "e2m1")
    w3_words, w3_scales = pack_weight(n((K, N)) / np.sqrt(K) / s, "e4m3")
    return {
        "tab_words": tab_words, "tab_scales": tab_scales,
        "offs": striped(np.random.permutation(T)[:S]),
        "w1": (n((K, H)) / np.sqrt(K) / s * u.T).astype(np.float32),
        "w2_words": w2_words, "w2_scales": w2_scales,
        "bt": (0.5 * n(H)).astype(np.float32),
        "gain": (np.exp(0.3 * n(H)) * u[:, 0]).astype(np.float32),
        "w3_words": w3_words, "w3_scales": w3_scales,
        "w4": (n((H, N)) / np.sqrt(H) / u).astype(np.float32),
    }

def reference(tab_words, tab_scales, offs, w1, w2_words, w2_scales, bt, gain, w3_words, w3_scales, w4):
    v = unpack_weight(tab_words, tab_scales, "e4m3")[:, unstriped(offs)]
    act = mxq(f64(w1), 0, "e4m3").T @ v
    peer = unpack_weight(w2_words, w2_scales, "e2m1").T @ v
    h = act - f64(gain)[:, None] * np.tanh(peer + f64(bt)[:, None])
    words, scales = planes(h)
    hq = mxq(h, 0, "e4m3")
    ring = mxq(f64(w4), 0, "e4m3").T @ hq
    direct = unpack_weight(w3_words, w3_scales, "e4m3").T @ v
    y = ring * direct
    return y, h, words, scales

@@ -1,0 +1,313 @@
+from contextlib import ExitStack
+
+import concourse.mybir as mybir
+
+K, T, S, H, N = 1024, 2048, 1024, 512, 384
+FLOPS = 2 * S * (2 * K * H + K * N + H * N)
+
+F32 = mybir.dt.float32
+BF16 = mybir.dt.bfloat16
+I32 = mybir.dt.int32
+U32 = mybir.dt.uint32
+U16 = mybir.dt.uint16
+U8 = mybir.dt.uint8
+FP8X4 = mybir.dt.float8_e4m3fn_x4
+FP4X4 = mybir.dt.float4_e2m1fn_x4
+MULT = mybir.AluOpType.mult
+ADD = mybir.AluOpType.add
+TANH = mybir.ActivationFunctionType.Tanh
+
+P = 128
+PACK = 4
+PASSES = K // (P * PACK)
+HALF = 512
+HALVES = S // HALF
+QUARTER = 256
+N_TILES = N // P
+QUADS = 4
+
+
+def tile_list_fraud_ring_cards_kernel(
+    tc, tab_words, tab_scales, offs, w1, w2_words, w2_scales, bt, gain, w3_words, w3_scales, w4,
+    out_0, out_1, out_2, out_3,
+):
+    nc = tc.nc
+    with ExitStack() as ctx:
+        keep = ctx.enter_context(tc.tile_pool(name="keep", bufs=1))
+        psum = ctx.enter_context(tc.psum_pool(name="psum", bufs=1))
+
+        def sb(name, shape, dtype, tag=None):
+            return keep.tile(shape, dtype, name=name, tag=tag or name, align_bytes=64)
+
+        def bank(b):
+            return psum.tile([P, HALF], F32, name="bank%d" % b)
+
+        offsets = keep.tile([P, S // 16], U16, name="offsets")
+        tab_sc = sb("tab_sc", [P, T], U8)
+        w2_sc_raw = sb("w2_sc_raw", [P, PASSES, H], U8)
+        w3_sc = sb("w3_sc", [P, PASSES, N], U8)
+        v_sc1 = sb("v_sc1", [P, S], U8)
+
+        tab_sc_rows = sb("tab_sc_rows", [P, T], U8)
+        warm = sb("warm", [P, 2], F32)
+        nc.gpsimd.memset(w3_sc[:].rearrange("p a c -> p (a c)").bitcast(I32), 0)
+        nc.vector.memset(w2_sc_raw[:].rearrange("p a c -> p (a c)").bitcast(I32), 0)
+        nc.vector.memset(warm[:, 0:1], 0.0)
+        nc.scalar.activation(warm[:, 1:2], warm[:, 0:1], TANH)
+        nc.vector.memset(tab_sc[:].bitcast(I32), 0)
+        nc.vector.memset(v_sc1[:].bitcast(I32), 0)
+
+        for q in range(QUADS):
+            nc.sync.dma_start(
+                out=tab_sc_rows[32 * q : 32 * q + 8, :].bitcast(I32),
+                in_=tab_scales[:, 4 * q : 4 * q + 4, :].bitcast(I32),
+            )
+        nc.sync.dma_start(offsets[:], offs)
+        w2_raw = sb("w2_raw", [P, PASSES, 2 * H], U8)
+        nc.sync.dma_start(out=w2_raw[:].bitcast(I32), in_=w2_words.rearrange("a p c -> p a c").bitcast(I32))
+        tab = []
+
+        def load_table(a, tag):
+            words = sb("tab%d" % a, [P, T], I32, tag=tag)
+            nc.sync.dma_start(out=words[:], in_=tab_words[a].rearrange("p t i -> p (t i)").bitcast(I32))
+            tab.append(words)
+
+        load_table(0, None)
+        w1_rows = [w1[512 * a : 512 * (a + 1), :].rearrange("(p j) c -> p j c", j=PACK) for a in range(PASSES)]
+        w1_raw0 = sb("w1_raw0", [P, PACK, H], F32)
+        nc.sync.dma_start(out=w1_raw0[:], in_=w1_rows[0])
+        for q in range(QUADS):
+            nc.sync.dma_start(
+                out=w2_sc_raw[32 * q : 32 * q + 4, :, :].bitcast(I32),
+                in_=w2_scales[:, 4 * q : 4 * q + 4, :].rearrange("a r c -> r a c").bitcast(I32),
+            )
+        bt_sb = sb("bt_sb", [P, PACK], F32)
+        gain_sb = sb("gain_sb", [P, PACK], F32)
+        nc.gpsimd.dma_start(out=bt_sb[:], in_=bt.rearrange("(p t) -> p t", t=PACK))
+        nc.gpsimd.dma_start(out=gain_sb[:], in_=gain.rearrange("(p t) -> p t", t=PACK))
+
+        for q in range(QUADS):
+            rows = slice(32 * q, 32 * q + 8)
+            nc.vector.tensor_copy(tab_sc[rows, :].bitcast(I32), tab_sc_rows[rows, :].bitcast(I32))
+        load_table(1, "tab_sc_rows")
+        v_sc = sb("v_sc", [P, S], U8)
+        nc.vector.tensor_copy(v_sc[:], tab_sc[:].indirect(offsets[:]))
+        nc.sync.dma_start(out=v_sc1[0:100, :].bitcast(I32), in_=v_sc[4:104, :].bitcast(I32))
+        w1_raw1 = sb("w1_raw1", [P, 2, PACK, H // 2], F32, tag="tab_sc")
+        for u in range(2):
+            nc.sync.dma_start(out=w1_raw1[:, u], in_=w1_rows[1][:, :, 256 * u : 256 * (u + 1)])
+        for q in range(QUADS):
+            nc.gpsimd.dma_start(
+                out=w3_sc[32 * q : 32 * q + 4, :, :].bitcast(I32),
+                in_=w3_scales[:, 4 * q : 4 * q + 4, :].rearrange("a r c -> r a c").bitcast(I32),
+            )
+        neg_gain = sb("neg_gain", [P, PACK], F32)
+        nc.gpsimd.tensor_scalar(neg_gain[:], gain_sb[:], -1.0, 0.0, MULT, ADD)
+
+        w2_codes = sb("w2_codes", [P, PASSES, 2 * H], U8)
+        nc.vector.tensor_copy(
+            w2_codes[:].bitcast(U16).rearrange("p a (t m) -> p a t m", t=PACK),
+            w2_raw[:].bitcast(U16).rearrange("p a (m t) -> p a t m", t=PACK),
+        )
+
+        w3_codes = sb("w3_codes", [P, PASSES, N], I32, tag="w2_raw")
+        nc.sync.dma_start(out=w3_codes[:], in_=w3_words.rearrange("a p c i -> p a (c i)").bitcast(I32))
+
+        v = {}
+
+        def gather(a, hf, words):
+            v[a, hf] = words[:, HALF * hf : HALF * (hf + 1)]
+            nc.vector.tensor_copy(v[a, hf], tab[a][:].bitcast(U32).indirect(offsets[:, 32 * hf : 32 * (hf + 1)]))
+
+        def v_plane(a, hf, shifted):
+            cols = slice(HALF * hf, HALF * (hf + 1))
+            if a == 0:
+                return v_sc[:, cols]
+            return v_sc1[:, cols] if shifted else v_sc[4:, cols]
+
+        v0 = sb("v0", [P, S], U32)
+        gather(0, 0, v0)
+        gather(0, 1, v0)
+        w4_raw = sb("w4_raw", [P, PACK, N], F32, tag="tab0")
+        nc.sync.dma_start(out=w4_raw[:], in_=w4.rearrange("(p j) n -> p j n", j=PACK))
+        w2_sc = sb("w2_sc", [P, PASSES, H], U8)
+        nc.vector.tensor_copy(
+            w2_sc[:].rearrange("p a (t m) -> p a t m", t=PACK),
+            w2_sc_raw[:].rearrange("p a (m t) -> p a t m", t=PACK),
+        )
+
+        def peer_pass(acc, a, hf, t):
+            nc.tensor.matmul_mx(
+                out=acc[:],
+                lhsT=w2_codes[:, a, 256 * t : 256 * (t + 1)].bitcast(FP4X4),
+                lhsT_scale=w2_sc[:, a, P * t : P * (t + 1)],
+                rhs=v[a, hf].bitcast(FP8X4),
+                rhs_scale=v_plane(a, hf, True),
+                start=(a == 0),
+                stop=(a == PASSES - 1),
+            )
+
+        th = {}
+
+        def tanh(acc, hf, t):
+            th[hf, t] = sb("th%d%d" % (hf, t), [P, HALF], F32)
+            nc.scalar.activation(th[hf, t][:], acc[:], TANH, bias=bt_sb[:, t : t + 1])
+
+        peer0 = [bank(t) for t in range(PACK)]
+        for t in range(PACK):
+            peer_pass(peer0[t], 0, 0, t)
+        peer1 = [bank(4 + t) for t in range(PACK)]
+        for t in range(PACK):
+            peer_pass(peer1[t], 0, 1, t)
+        v1 = sb("v1", [P, S], U32, tag="w2_sc_raw")
+        gather(1, 0, v1)
+        for t in range(PACK):
+            peer_pass(peer0[t], 1, 0, t)
+        gather(1, 1, v1)
+        for t in range(PACK):
+            peer_pass(peer1[t], 1, 1, t)
+
+        w1_bf = [sb("w1_bf%d" % a, [P, PACK * H], BF16) for a in range(PASSES)]
+        w1_codes = [sb("w1_codes%d" % a, [P, H], U32) for a in range(PASSES)]
+        w1_sc = [sb("w1_sc%d" % a, [P, H], U8) for a in range(PASSES)]
+
+        def w1_views(a, raw, m0, m1, raw_m0):
+            dst = w1_bf[a][:].rearrange("p (t m j) -> p m j t", t=PACK, j=PACK)[:, m0:m1]
+            src = raw.rearrange("p j (m t) -> p m j t", t=PACK)[:, m0 - raw_m0 : m1 - raw_m0]
+            return dst, src
+
+        nc.scalar.copy(*w1_views(0, w1_raw0[:], 0, P, 0))
+        nc.scalar.copy(*w1_views(1, w1_raw1[:, 0], 0, 64, 0))
+        nc.vector.quantize_mx(out=w1_codes[0][:].bitcast(FP8X4), scales=w1_sc[0][:], in_=w1_bf[0][:])
+        nc.vector.tensor_copy(*w1_views(1, w1_raw1[:, 1], 64, P, 64))
+        for t in range(PACK):
+            tanh(peer0[t], 0, t)
+
+        def act_pass(acc, a, hf, t):
+            nc.tensor.matmul_mx(
+                out=acc[:],
+                lhsT=w1_codes[a][:, P * t : P * (t + 1)].bitcast(FP8X4),
+                lhsT_scale=w1_sc[a][:, P * t : P * (t + 1)],
+                rhs=v[a, hf].bitcast(FP8X4),
+                rhs_scale=v_plane(a, hf, False),
+                start=(a == 0),
+                stop=(a == PASSES - 1),
+            )
+
+        act0 = [bank(t) for t in range(PACK)]
+        for t in range(PACK):
+            nc.vector.quantize_mx(
+                out=w1_codes[1][:, P * t : P * (t + 1)].bitcast(FP8X4),
+                scales=w1_sc[1][:, P * t : P * (t + 1)],
+                in_=w1_bf[1][:, HALF * t : HALF * (t + 1)],
+            )
+        for t in range(PACK):
+            for a in range(PASSES):
+                act_pass(act0[t], a, 0, t)
+        for t in range(PACK):
+            tanh(peer1[t], 1, t)
+
+        h = [sb("h%d" % hf, [P, PACK, HALF], F32) for hf in range(HALVES)]
+        h_rows = out_1.rearrange("(p t) j -> p t j", t=PACK)
+
+        def subtract(acc, hf, t):
+            nc.vector.scalar_tensor_tensor(h[hf][:, t, :], th[hf, t][:], neg_gain[:, t : t + 1], acc[:], MULT, ADD)
+            nc.sync.dma_start(out=h_rows[:, t, HALF * hf : HALF * (hf + 1)], in_=h[hf][:, t, :])
+
+        for t in range(PACK):
+            subtract(act0[t], 0, t)
+
+        w4_bf = sb("w4_bf", [P, PACK * N], BF16)
+        w4_codes = sb("w4_codes", [P, N], U32)
+        w4_sc = sb("w4_sc", [P, N], U8)
+        w4_dst = w4_bf[:].rearrange("p (c i j) -> p c j i", i=4, j=PACK)
+        w4_src = w4_raw[:].rearrange("p j (c i) -> p c j i", i=4)
+
+        act1 = [bank(4 + t) for t in range(PACK)]
+        for t in range(PACK):
+            for a in range(PASSES):
+                act_pass(act1[t], a, 1, t)
+
+        h_bf = [sb("h_bf%d" % c, [P, PACK * QUARTER], BF16) for c in range(4)]
+        h_codes = [sb("h_codes%d" % hf, [P, HALF], U32) for hf in range(HALVES)]
+        h_sc = sb("h_sc", [P, S], U8)
+
+        def h_views(c):
+            hf, u = divmod(c, 2)
+            dst = h_bf[c][:].rearrange("p (c i t) -> p c t i", i=4, t=PACK)
+            src = h[hf][:, :, QUARTER * u : QUARTER * (u + 1)].rearrange("p t (c i) -> p c t i", i=4)
+            return dst, src
+
+        def h_quantize(c):
+            hf, u = divmod(c, 2)
+            nc.vector.quantize_mx(
+                out=h_codes[hf][:, QUARTER * u : QUARTER * (u + 1)].bitcast(FP8X4),
+                scales=h_sc[:, QUARTER * c : QUARTER * (c + 1)],
+                in_=h_bf[c][:],
+            )
+
+        for c in (0, 1):
+            nc.scalar.copy(*h_views(c))
+        for t in range(PACK):
+            subtract(act1[t], 1, t)
+
+        direct = {}
+
+        def direct_tile(b, hf, n):
+            acc = bank(b)
+            for a in range(PASSES):
+                nc.tensor.matmul_mx(
+                    out=acc[:],
+                    lhsT=w3_codes[:, a, P * n : P * (n + 1)].bitcast(FP8X4),
+                    lhsT_scale=w3_sc[:, a, P * n : P * (n + 1)],
+                    rhs=v[a, hf].bitcast(FP8X4),
+                    rhs_scale=v_plane(a, hf, False),
+                    start=(a == 0),
+                    stop=(a == PASSES - 1),
+                )
+            direct[hf, n] = sb("direct%d%d" % (hf, n), [P, HALF], F32)
+            nc.scalar.copy(direct[hf, n][:], acc[:])
+
+        def ring_tile(b, hf, n):
+            acc = bank(b)
+            nc.tensor.matmul_mx(
+                out=acc[:],
+                lhsT=w4_codes[:, P * n : P * (n + 1)].bitcast(FP8X4),
+                lhsT_scale=w4_sc[:, P * n : P * (n + 1)],
+                rhs=h_codes[hf][:].bitcast(FP8X4),
+                rhs_scale=h_sc[:, HALF * hf : HALF * (hf + 1)],
+                start=True,
+                stop=True,
+            )
+            y = sb("y%d%d" % (hf, n), [P, HALF], F32)
+            nc.vector.tensor_tensor(y[:], acc[:], direct[hf, n][:], MULT)
+            nc.sync.dma_start(out=out_0[P * n : P * (n + 1), HALF * hf : HALF * (hf + 1)], in_=y[:])
+
+        code_rows = out_2[0].rearrange("p m t -> p (m t)").bitcast(I32)
+
+        def store_codes(hf):
+            nc.sync.dma_start(out=code_rows[:, HALF * hf : HALF * (hf + 1)], in_=h_codes[hf][:].bitcast(I32))
+
+        for n in range(N_TILES):
+            direct_tile(n, 0, n)
+        nc.vector.tensor_copy(w4_dst, w4_src)
+        nc.vector.tensor_copy(*h_views(3))
+        for c0, c1 in ((0, 256), (256, N)):
+            nc.vector.quantize_mx(
+                out=w4_codes[:, c0:c1].bitcast(FP8X4), scales=w4_sc[:, c0:c1], in_=w4_bf[:, PACK * c0 : PACK * c1]
+            )
+        h_quantize(0)
+        h_quantize(1)
+        store_codes(0)
+        nc.scalar.copy(*h_views(2))
+        for n, b in enumerate((3, 0, 1)):
+            ring_tile(b, 0, n)
+        for n in range(N_TILES):
+            direct_tile(4 + n, 1, n)
+        h_quantize(2)
+        h_quantize(3)
+        store_codes(1)
+        for q in range(QUADS):
+            nc.sync.dma_start(out=out_3[0][4 * q : 4 * q + 4, :].bitcast(I32), in_=h_sc[32 * q : 32 * q + 4, :].bitcast(I32))
+        for n, b in enumerate((7, 2, 3)):
+            ring_tile(b, 1, n)

@@ -34,23 +34,25 @@ def tile_list_fraud_ring_cards_kernel(
     nc = tc.nc
     with ExitStack() as ctx:
         keep = ctx.enter_context(tc.tile_pool(name="keep", bufs=1))
+        shared = ctx.enter_context(tc.tile_pool(name="shared", bufs=1))
         psum = ctx.enter_context(tc.psum_pool(name="psum", bufs=1))
 
         def sb(name, shape, dtype, tag=None):
             return keep.tile(shape, dtype, name=name, tag=tag or name, align_bytes=64)
 
+        def placed(name, shape, dtype, offset):
+            return shared.tile(shape, dtype, name=name, offset=offset, align_bytes=64)
+
         def bank(b):
             return psum.tile([P, HALF], F32, name="bank%d" % b)
 
         offsets = keep.tile([P, S // 16], U16, name="offsets")
-        tab_sc = sb("tab_sc", [P, T], U8)
+        tab_sc = placed("tab_sc", [P, T], U8, 8192 - 1024)
         w2_sc_raw = sb("w2_sc_raw", [P, PASSES, H], U8)
-        w3_sc = sb("w3_sc", [P, PASSES, N], U8)
         v_sc1 = sb("v_sc1", [P, S], U8)
 
         tab_sc_rows = sb("tab_sc_rows", [P, T], U8)
         warm = sb("warm", [P, 2], F32)
-        nc.gpsimd.memset(w3_sc[:].rearrange("p a c -> p (a c)").bitcast(I32), 0)
         nc.vector.memset(w2_sc_raw[:].rearrange("p a c -> p (a c)").bitcast(I32), 0)
         nc.vector.memset(warm[:, 0:1], 0.0)
         nc.scalar.activation(warm[:, 1:2], warm[:, 0:1], TANH)
@@ -73,36 +75,32 @@ def tile_list_fraud_ring_cards_kernel(
             tab.append(words)
 
         load_table(0, None)
-        w1_rows = [w1[512 * a : 512 * (a + 1), :].rearrange("(p j) c -> p j c", j=PACK) for a in range(PASSES)]
-        w1_raw0 = sb("w1_raw0", [P, PACK, H], F32)
-        nc.sync.dma_start(out=w1_raw0[:], in_=w1_rows[0])
+        bt_sb = sb("bt_sb", [P, PACK], F32)
+        gain_sb = sb("gain_sb", [P, PACK], F32)
+        nc.sync.dma_start(out=bt_sb[:], in_=bt.rearrange("(p t) -> p t", t=PACK))
+        nc.sync.dma_start(out=gain_sb[:], in_=gain.rearrange("(p t) -> p t", t=PACK))
         for q in range(QUADS):
             nc.sync.dma_start(
                 out=w2_sc_raw[32 * q : 32 * q + 4, :, :].bitcast(I32),
                 in_=w2_scales[:, 4 * q : 4 * q + 4, :].rearrange("a r c -> r a c").bitcast(I32),
             )
-        bt_sb = sb("bt_sb", [P, PACK], F32)
-        gain_sb = sb("gain_sb", [P, PACK], F32)
-        nc.gpsimd.dma_start(out=bt_sb[:], in_=bt.rearrange("(p t) -> p t", t=PACK))
-        nc.gpsimd.dma_start(out=gain_sb[:], in_=gain.rearrange("(p t) -> p t", t=PACK))
+        w1_rows = [w1[512 * a : 512 * (a + 1), :].rearrange("(p j) c -> p j c", j=PACK) for a in range(PASSES)]
+        load_table(1, "warm")
+        neg_gain = sb("neg_gain", [P, PACK], F32)
+        nc.scalar.mul(neg_gain[:], gain_sb[:], -1.0)
 
         for q in range(QUADS):
             rows = slice(32 * q, 32 * q + 8)
             nc.vector.tensor_copy(tab_sc[rows, :].bitcast(I32), tab_sc_rows[rows, :].bitcast(I32))
-        load_table(1, "tab_sc_rows")
         v_sc = sb("v_sc", [P, S], U8)
         nc.vector.tensor_copy(v_sc[:], tab_sc[:].indirect(offsets[:]))
         nc.sync.dma_start(out=v_sc1[0:100, :].bitcast(I32), in_=v_sc[4:104, :].bitcast(I32))
-        w1_raw1 = sb("w1_raw1", [P, 2, PACK, H // 2], F32, tag="tab_sc")
+        w1_raw0 = placed("w1_raw0", [P, PACK, H], F32, 0)
+        nc.sync.dma_start(out=w1_raw0[:], in_=w1_rows[0])
+        w1_flat1 = placed("w1_flat1", [P, PACK * H], F32, 8192)
+        w1_raw1 = [w1_flat1[:, 1024 * u : 1024 * (u + 1)].rearrange("p (j c) -> p j c", j=PACK) for u in range(2)]
         for u in range(2):
-            nc.sync.dma_start(out=w1_raw1[:, u], in_=w1_rows[1][:, :, 256 * u : 256 * (u + 1)])
-        for q in range(QUADS):
-            nc.gpsimd.dma_start(
-                out=w3_sc[32 * q : 32 * q + 4, :, :].bitcast(I32),
-                in_=w3_scales[:, 4 * q : 4 * q + 4, :].rearrange("a r c -> r a c").bitcast(I32),
-            )
-        neg_gain = sb("neg_gain", [P, PACK], F32)
-        nc.gpsimd.tensor_scalar(neg_gain[:], gain_sb[:], -1.0, 0.0, MULT, ADD)
+            nc.sync.dma_start(out=w1_raw1[u], in_=w1_rows[1][:, :, 256 * u : 256 * (u + 1)])
 
         w2_codes = sb("w2_codes", [P, PASSES, 2 * H], U8)
         nc.vector.tensor_copy(
@@ -110,13 +108,18 @@ def tile_list_fraud_ring_cards_kernel(
             w2_raw[:].bitcast(U16).rearrange("p a (m t) -> p a t m", t=PACK),
         )
 
-        w3_codes = sb("w3_codes", [P, PASSES, N], I32, tag="w2_raw")
-        nc.sync.dma_start(out=w3_codes[:], in_=w3_words.rearrange("a p c i -> p a (c i)").bitcast(I32))
+        w3_sc = sb("w3_sc", [P, PASSES, N], U8, tag="w2_raw")
+        nc.gpsimd.memset(w3_sc[:].rearrange("p a c -> p (a c)").bitcast(I32), 0)
+        for q in range(QUADS):
+            nc.sync.dma_start(
+                out=w3_sc[32 * q : 32 * q + 4, :, :].bitcast(I32),
+                in_=w3_scales[:, 4 * q : 4 * q + 4, :].rearrange("a r c -> r a c").bitcast(I32),
+            )
 
         v = {}
 
-        def gather(a, hf, words):
-            v[a, hf] = words[:, HALF * hf : HALF * (hf + 1)]
+        def gather(a, hf, tag=None):
+            v[a, hf] = sb("v%d%d" % (a, hf), [P, HALF], U32, tag=tag)[:]
             nc.vector.tensor_copy(v[a, hf], tab[a][:].bitcast(U32).indirect(offsets[:, 32 * hf : 32 * (hf + 1)]))
 
         def v_plane(a, hf, shifted):
@@ -125,16 +128,15 @@ def tile_list_fraud_ring_cards_kernel(
                 return v_sc[:, cols]
             return v_sc1[:, cols] if shifted else v_sc[4:, cols]
 
-        v0 = sb("v0", [P, S], U32)
-        gather(0, 0, v0)
-        gather(0, 1, v0)
-        w4_raw = sb("w4_raw", [P, PACK, N], F32, tag="tab0")
-        nc.sync.dma_start(out=w4_raw[:], in_=w4.rearrange("(p j) n -> p j n", j=PACK))
+        gather(0, 0)
         w2_sc = sb("w2_sc", [P, PASSES, H], U8)
         nc.vector.tensor_copy(
             w2_sc[:].rearrange("p a (t m) -> p a t m", t=PACK),
             w2_sc_raw[:].rearrange("p a (m t) -> p a t m", t=PACK),
         )
+        gather(0, 1, "w2_sc_raw")
+        w3_codes = sb("w3_codes", [P, PASSES, N], I32, tag="tab0")
+        nc.sync.dma_start(out=w3_codes[:], in_=w3_words.rearrange("a p c i -> p a (c i)").bitcast(I32))
 
         def peer_pass(acc, a, hf, t):
             nc.tensor.matmul_mx(
@@ -150,8 +152,7 @@ def tile_list_fraud_ring_cards_kernel(
         th = {}
 
         def tanh(acc, hf, t):
-            th[hf, t] = sb("th%d%d" % (hf, t), [P, HALF], F32)
-            nc.scalar.activation(th[hf, t][:], acc[:], TANH, bias=bt_sb[:, t : t + 1])
+            nc.scalar.activation(th[hf][:, t, :], acc[:], TANH, bias=bt_sb[:, t : t + 1])
 
         peer0 = [bank(t) for t in range(PACK)]
         for t in range(PACK):
@@ -159,14 +160,6 @@ def tile_list_fraud_ring_cards_kernel(
         peer1 = [bank(4 + t) for t in range(PACK)]
         for t in range(PACK):
             peer_pass(peer1[t], 0, 1, t)
-        v1 = sb("v1", [P, S], U32, tag="w2_sc_raw")
-        gather(1, 0, v1)
-        for t in range(PACK):
-            peer_pass(peer0[t], 1, 0, t)
-        gather(1, 1, v1)
-        for t in range(PACK):
-            peer_pass(peer1[t], 1, 1, t)
-
         w1_bf = [sb("w1_bf%d" % a, [P, PACK * H], BF16) for a in range(PASSES)]
         w1_codes = [sb("w1_codes%d" % a, [P, H], U32) for a in range(PASSES)]
         w1_sc = [sb("w1_sc%d" % a, [P, H], U8) for a in range(PASSES)]
@@ -176,10 +169,20 @@ def tile_list_fraud_ring_cards_kernel(
             src = raw.rearrange("p j (m t) -> p m j t", t=PACK)[:, m0 - raw_m0 : m1 - raw_m0]
             return dst, src
 
+        gather(1, 0)
+        for t in range(PACK):
+            peer_pass(peer0[t], 1, 0, t)
+        gather(1, 1)
+        w4_raw = sb("w4_raw", [P, PACK, N], F32, tag="warm")
+        nc.sync.dma_start(out=w4_raw[:], in_=w4.rearrange("(p j) n -> p j n", j=PACK))
+        for t in range(PACK):
+            peer_pass(peer1[t], 1, 1, t)
         nc.scalar.copy(*w1_views(0, w1_raw0[:], 0, P, 0))
-        nc.scalar.copy(*w1_views(1, w1_raw1[:, 0], 0, 64, 0))
+        nc.vector.tensor_copy(*w1_views(1, w1_raw1[0], 0, 64, 0))
+        nc.vector.tensor_copy(*w1_views(1, w1_raw1[1], 64, P, 64))
         nc.vector.quantize_mx(out=w1_codes[0][:].bitcast(FP8X4), scales=w1_sc[0][:], in_=w1_bf[0][:])
-        nc.vector.tensor_copy(*w1_views(1, w1_raw1[:, 1], 64, P, 64))
+        th[0] = placed("th0", [P, PACK, HALF], F32, 0)
+        th[1] = placed("th1", [P, PACK, HALF], F32, 8192)
         for t in range(PACK):
             tanh(peer0[t], 0, t)
 
@@ -195,11 +198,9 @@ def tile_list_fraud_ring_cards_kernel(
             )
 
         act0 = [bank(t) for t in range(PACK)]
-        for t in range(PACK):
+        for c0, c1 in ((0, P), (P, 2 * P), (2 * P, H)):
             nc.vector.quantize_mx(
-                out=w1_codes[1][:, P * t : P * (t + 1)].bitcast(FP8X4),
-                scales=w1_sc[1][:, P * t : P * (t + 1)],
-                in_=w1_bf[1][:, HALF * t : HALF * (t + 1)],
+                out=w1_codes[1][:, c0:c1].bitcast(FP8X4), scales=w1_sc[1][:, c0:c1], in_=w1_bf[1][:, PACK * c0 : PACK * c1]
             )
         for t in range(PACK):
             for a in range(PASSES):
@@ -211,7 +212,7 @@ def tile_list_fraud_ring_cards_kernel(
         h_rows = out_1.rearrange("(p t) j -> p t j", t=PACK)
 
         def subtract(acc, hf, t):
-            nc.vector.scalar_tensor_tensor(h[hf][:, t, :], th[hf, t][:], neg_gain[:, t : t + 1], acc[:], MULT, ADD)
+            nc.vector.scalar_tensor_tensor(h[hf][:, t, :], th[hf][:, t, :], neg_gain[:, t : t + 1], acc[:], MULT, ADD)
             nc.sync.dma_start(out=h_rows[:, t, HALF * hf : HALF * (hf + 1)], in_=h[hf][:, t, :])
 
         for t in range(PACK):
@@ -222,28 +223,28 @@ def tile_list_fraud_ring_cards_kernel(
         w4_sc = sb("w4_sc", [P, N], U8)
         w4_dst = w4_bf[:].rearrange("p (c i j) -> p c j i", i=4, j=PACK)
         w4_src = w4_raw[:].rearrange("p j (c i) -> p c j i", i=4)
+        nc.scalar.copy(w4_dst[:, 0:64], w4_src[:, 0:64])
 
         act1 = [bank(4 + t) for t in range(PACK)]
         for t in range(PACK):
             for a in range(PASSES):
                 act_pass(act1[t], a, 1, t)
 
-        h_bf = [sb("h_bf%d" % c, [P, PACK * QUARTER], BF16) for c in range(4)]
+        h_bf = [sb("h_bf%d" % hf, [P, PACK * HALF], BF16) for hf in range(HALVES)]
         h_codes = [sb("h_codes%d" % hf, [P, HALF], U32) for hf in range(HALVES)]
         h_sc = sb("h_sc", [P, S], U8)
 
         def h_views(c):
             hf, u = divmod(c, 2)
-            dst = h_bf[c][:].rearrange("p (c i t) -> p c t i", i=4, t=PACK)
+            dst = h_bf[hf][:, PACK * QUARTER * u : PACK * QUARTER * (u + 1)].rearrange("p (c i t) -> p c t i", i=4, t=PACK)
             src = h[hf][:, :, QUARTER * u : QUARTER * (u + 1)].rearrange("p t (c i) -> p c t i", i=4)
             return dst, src
 
-        def h_quantize(c):
-            hf, u = divmod(c, 2)
+        def h_quantize(hf):
             nc.vector.quantize_mx(
-                out=h_codes[hf][:, QUARTER * u : QUARTER * (u + 1)].bitcast(FP8X4),
-                scales=h_sc[:, QUARTER * c : QUARTER * (c + 1)],
-                in_=h_bf[c][:],
+                out=h_codes[hf][:].bitcast(FP8X4),
+                scales=h_sc[:, HALF * hf : HALF * (hf + 1)],
+                in_=h_bf[hf][:],
             )
 
         for c in (0, 1):
@@ -254,6 +255,8 @@ def tile_list_fraud_ring_cards_kernel(
         direct = {}
 
         def direct_tile(b, hf, n):
+            if n == 0:
+                direct[hf] = sb("direct%d" % hf, [P, N_TILES, HALF], F32, tag="h%d" % hf)
             acc = bank(b)
             for a in range(PASSES):
                 nc.tensor.matmul_mx(
@@ -265,8 +268,7 @@ def tile_list_fraud_ring_cards_kernel(
                     start=(a == 0),
                     stop=(a == PASSES - 1),
                 )
-            direct[hf, n] = sb("direct%d%d" % (hf, n), [P, HALF], F32)
-            nc.scalar.copy(direct[hf, n][:], acc[:])
+            nc.scalar.copy(direct[hf][:, n, :], acc[:])
 
         def ring_tile(b, hf, n):
             acc = bank(b)
@@ -280,7 +282,7 @@ def tile_list_fraud_ring_cards_kernel(
                 stop=True,
             )
             y = sb("y%d%d" % (hf, n), [P, HALF], F32)
-            nc.vector.tensor_tensor(y[:], acc[:], direct[hf, n][:], MULT)
+            nc.vector.tensor_tensor(y[:], acc[:], direct[hf][:, n, :], MULT)
             nc.sync.dma_start(out=out_0[P * n : P * (n + 1), HALF * hf : HALF * (hf + 1)], in_=y[:])
 
         code_rows = out_2[0].rearrange("p m t -> p (m t)").bitcast(I32)
@@ -290,22 +292,20 @@ def tile_list_fraud_ring_cards_kernel(
 
         for n in range(N_TILES):
             direct_tile(n, 0, n)
-        nc.vector.tensor_copy(w4_dst, w4_src)
-        nc.vector.tensor_copy(*h_views(3))
+        nc.vector.tensor_copy(w4_dst[:, 64:96], w4_src[:, 64:96])
         for c0, c1 in ((0, 256), (256, N)):
             nc.vector.quantize_mx(
                 out=w4_codes[:, c0:c1].bitcast(FP8X4), scales=w4_sc[:, c0:c1], in_=w4_bf[:, PACK * c0 : PACK * c1]
             )
         h_quantize(0)
-        h_quantize(1)
         store_codes(0)
         nc.scalar.copy(*h_views(2))
+        nc.vector.tensor_copy(*h_views(3))
         for n, b in enumerate((3, 0, 1)):
             ring_tile(b, 0, n)
         for n in range(N_TILES):
             direct_tile(4 + n, 1, n)
-        h_quantize(2)
-        h_quantize(3)
+        h_quantize(1)
         store_codes(1)
         for q in range(QUADS):
             nc.sync.dma_start(out=out_3[0][4 * q : 4 * q + 4, :].bitcast(I32), in_=h_sc[32 * q : 32 * q + 4, :].bitcast(I32))

@@ -34,36 +34,31 @@ def tile_list_fraud_ring_cards_kernel(
     nc = tc.nc
     with ExitStack() as ctx:
         keep = ctx.enter_context(tc.tile_pool(name="keep", bufs=1))
-        shared = ctx.enter_context(tc.tile_pool(name="shared", bufs=1))
         psum = ctx.enter_context(tc.psum_pool(name="psum", bufs=1))
 
         def sb(name, shape, dtype, tag=None):
             return keep.tile(shape, dtype, name=name, tag=tag or name, align_bytes=64)
 
-        def placed(name, shape, dtype, offset):
-            return shared.tile(shape, dtype, name=name, offset=offset, align_bytes=64)
-
         def bank(b):
             return psum.tile([P, HALF], F32, name="bank%d" % b)
 
         offsets = keep.tile([P, S // 16], U16, name="offsets")
-        tab_sc = placed("tab_sc", [P, T], U8, 8192 - 1024)
-        w2_sc_raw = sb("w2_sc_raw", [P, PASSES, H], U8)
-        v_sc1 = sb("v_sc1", [P, S], U8)
+        w2_sc_raw = sb("w2_sc_raw", [P, H], U8)
+        tab_sc = sb("tab_sc", [P, T], U8)
+        for rows in (w2_sc_raw, tab_sc):
+            nc.vector.memset(rows[0:96, :].bitcast(I32), 0)
+        w2_sc = sb("w2_sc", [P, PASSES * H], U8)
+        nc.gpsimd.memset(w2_sc[:].bitcast(I32), 0)
+        v_sc = sb("v_sc", [P, PASSES * S], U8)
+        nc.gpsimd.memset(v_sc[:].bitcast(I32), 0)
 
-        tab_sc_rows = sb("tab_sc_rows", [P, T], U8)
-        warm = sb("warm", [P, 2], F32)
-        nc.vector.memset(w2_sc_raw[:].rearrange("p a c -> p (a c)").bitcast(I32), 0)
-        nc.vector.memset(warm[:, 0:1], 0.0)
-        nc.scalar.activation(warm[:, 1:2], warm[:, 0:1], TANH)
-        nc.vector.memset(tab_sc[:].bitcast(I32), 0)
-        nc.vector.memset(v_sc1[:].bitcast(I32), 0)
+        def move_to_planes(queue, planes, rows):
+            for q in range(QUADS):
+                queue.dma_start(out=planes[32 * q : 32 * q + 4, :].bitcast(I32), in_=rows[96 + 8 * q : 104 + 8 * q, :].bitcast(I32))
 
-        for q in range(QUADS):
-            nc.sync.dma_start(
-                out=tab_sc_rows[32 * q : 32 * q + 8, :].bitcast(I32),
-                in_=tab_scales[:, 4 * q : 4 * q + 4, :].bitcast(I32),
-            )
+        nc.sync.dma_start(out=w2_sc_raw[96:128, :].bitcast(I32), in_=w2_scales.rearrange("a q c -> q a c").bitcast(I32))
+
+        nc.sync.dma_start(out=tab_sc[96:128, :].bitcast(I32), in_=tab_scales.rearrange("a q t -> q a t").bitcast(I32))
         nc.sync.dma_start(offsets[:], offs)
         w2_raw = sb("w2_raw", [P, PASSES, 2 * H], U8)
         nc.sync.dma_start(out=w2_raw[:].bitcast(I32), in_=w2_words.rearrange("a p c -> p a c").bitcast(I32))
@@ -75,45 +70,43 @@ def tile_list_fraud_ring_cards_kernel(
             tab.append(words)
 
         load_table(0, None)
-        bt_sb = sb("bt_sb", [P, PACK], F32)
         gain_sb = sb("gain_sb", [P, PACK], F32)
-        nc.sync.dma_start(out=bt_sb[:], in_=bt.rearrange("(p t) -> p t", t=PACK))
         nc.sync.dma_start(out=gain_sb[:], in_=gain.rearrange("(p t) -> p t", t=PACK))
-        for q in range(QUADS):
-            nc.sync.dma_start(
-                out=w2_sc_raw[32 * q : 32 * q + 4, :, :].bitcast(I32),
-                in_=w2_scales[:, 4 * q : 4 * q + 4, :].rearrange("a r c -> r a c").bitcast(I32),
-            )
-        w1_rows = [w1[512 * a : 512 * (a + 1), :].rearrange("(p j) c -> p j c", j=PACK) for a in range(PASSES)]
-        load_table(1, "warm")
+        bt_sb = sb("bt_sb", [P, PACK], F32)
+        nc.sync.dma_start(out=bt_sb[:], in_=bt.rearrange("(p t) -> p t", t=PACK))
         neg_gain = sb("neg_gain", [P, PACK], F32)
         nc.scalar.mul(neg_gain[:], gain_sb[:], -1.0)
 
-        for q in range(QUADS):
-            rows = slice(32 * q, 32 * q + 8)
-            nc.vector.tensor_copy(tab_sc[rows, :].bitcast(I32), tab_sc_rows[rows, :].bitcast(I32))
-        v_sc = sb("v_sc", [P, S], U8)
-        nc.vector.tensor_copy(v_sc[:], tab_sc[:].indirect(offsets[:]))
-        nc.sync.dma_start(out=v_sc1[0:100, :].bitcast(I32), in_=v_sc[4:104, :].bitcast(I32))
-        w1_raw0 = placed("w1_raw0", [P, PACK, H], F32, 0)
-        nc.sync.dma_start(out=w1_raw0[:], in_=w1_rows[0])
-        w1_flat1 = placed("w1_flat1", [P, PACK * H], F32, 8192)
-        w1_raw1 = [w1_flat1[:, 1024 * u : 1024 * (u + 1)].rearrange("p (j c) -> p j c", j=PACK) for u in range(2)]
-        for u in range(2):
-            nc.sync.dma_start(out=w1_raw1[u], in_=w1_rows[1][:, :, 256 * u : 256 * (u + 1)])
+        w2_sc_dealt = sb("w2_sc_dealt", [P, H], U8)
+        nc.vector.tensor_copy(
+            w2_sc_dealt[:].rearrange("p (t m) -> p t m", t=PACK), w2_sc_raw[:].rearrange("p (m t) -> p t m", t=PACK)
+        )
+        move_to_planes(nc.sync, w2_sc, w2_sc_dealt)
+        load_table(1, "w2_sc_raw")
+        picked_sc = sb("picked_sc", [P, S], U8)
+        nc.vector.tensor_copy(picked_sc[:], tab_sc[:].indirect(offsets[:]))
+        move_to_planes(nc.sync, v_sc, picked_sc)
 
         w2_codes = sb("w2_codes", [P, PASSES, 2 * H], U8)
         nc.vector.tensor_copy(
             w2_codes[:].bitcast(U16).rearrange("p a (t m) -> p a t m", t=PACK),
             w2_raw[:].bitcast(U16).rearrange("p a (m t) -> p a t m", t=PACK),
         )
+        w1_raw = []
 
-        w3_sc = sb("w3_sc", [P, PASSES, N], U8, tag="w2_raw")
-        nc.gpsimd.memset(w3_sc[:].rearrange("p a c -> p (a c)").bitcast(I32), 0)
+        def load_w1(a, tag):
+            raw = sb("w1_raw%d" % a, [P, PACK, H], F32, tag=tag)
+            nc.sync.dma_start(out=raw[:], in_=w1[512 * a : 512 * (a + 1), :].rearrange("(p j) c -> p j c", j=PACK))
+            w1_raw.append(raw)
+
+        load_w1(0, "tab_sc")
+        load_w1(1, "w2_raw")
+        w3_sc = sb("w3_sc", [P, N], U8, tag="picked_sc")
+        nc.gpsimd.memset(w3_sc[:].bitcast(I32), 0)
         for q in range(QUADS):
-            nc.sync.dma_start(
-                out=w3_sc[32 * q : 32 * q + 4, :, :].bitcast(I32),
-                in_=w3_scales[:, 4 * q : 4 * q + 4, :].rearrange("a r c -> r a c").bitcast(I32),
+            nc.scalar.dma_start(
+                out=w3_sc[32 * q + 8 : 32 * q + 16, :].bitcast(I32),
+                in_=w3_scales[:, 4 * q : 4 * q + 4, :].bitcast(I32),
             )
 
         v = {}
@@ -122,153 +115,101 @@ def tile_list_fraud_ring_cards_kernel(
             v[a, hf] = sb("v%d%d" % (a, hf), [P, HALF], U32, tag=tag)[:]
             nc.vector.tensor_copy(v[a, hf], tab[a][:].bitcast(U32).indirect(offsets[:, 32 * hf : 32 * (hf + 1)]))
 
-        def v_plane(a, hf, shifted):
-            cols = slice(HALF * hf, HALF * (hf + 1))
-            if a == 0:
-                return v_sc[:, cols]
-            return v_sc1[:, cols] if shifted else v_sc[4:, cols]
+        def v_plane(a, hf):
+            return v_sc[:, S * a + HALF * hf : S * a + HALF * (hf + 1)]
 
-        gather(0, 0)
-        w2_sc = sb("w2_sc", [P, PASSES, H], U8)
-        nc.vector.tensor_copy(
-            w2_sc[:].rearrange("p a (t m) -> p a t m", t=PACK),
-            w2_sc_raw[:].rearrange("p a (m t) -> p a t m", t=PACK),
-        )
-        gather(0, 1, "w2_sc_raw")
-        w3_codes = sb("w3_codes", [P, PASSES, N], I32, tag="tab0")
-        nc.sync.dma_start(out=w3_codes[:], in_=w3_words.rearrange("a p c i -> p a (c i)").bitcast(I32))
+        def first_stage(acc, codes, scales, a, hf, first=0):
+            nc.tensor.matmul_mx(
+                out=acc[:], lhsT=codes, lhsT_scale=scales, rhs=v[a, hf].bitcast(FP8X4), rhs_scale=v_plane(a, hf),
+                start=(a == first), stop=(a != first),
+            )
 
         def peer_pass(acc, a, hf, t):
-            nc.tensor.matmul_mx(
-                out=acc[:],
-                lhsT=w2_codes[:, a, 256 * t : 256 * (t + 1)].bitcast(FP4X4),
-                lhsT_scale=w2_sc[:, a, P * t : P * (t + 1)],
-                rhs=v[a, hf].bitcast(FP8X4),
-                rhs_scale=v_plane(a, hf, True),
-                start=(a == 0),
-                stop=(a == PASSES - 1),
-            )
+            first_stage(acc, w2_codes[:, a, 256 * t : 256 * (t + 1)].bitcast(FP4X4), w2_sc[:, H * a + P * t : H * a + P * (t + 1)], a, hf, hf)
 
-        th = {}
-
-        def tanh(acc, hf, t):
-            nc.scalar.activation(th[hf][:, t, :], acc[:], TANH, bias=bt_sb[:, t : t + 1])
-
-        peer0 = [bank(t) for t in range(PACK)]
-        for t in range(PACK):
-            peer_pass(peer0[t], 0, 0, t)
-        peer1 = [bank(4 + t) for t in range(PACK)]
-        for t in range(PACK):
-            peer_pass(peer1[t], 0, 1, t)
-        w1_bf = [sb("w1_bf%d" % a, [P, PACK * H], BF16) for a in range(PASSES)]
-        w1_codes = [sb("w1_codes%d" % a, [P, H], U32) for a in range(PASSES)]
-        w1_sc = [sb("w1_sc%d" % a, [P, H], U8) for a in range(PASSES)]
-
-        def w1_views(a, raw, m0, m1, raw_m0):
-            dst = w1_bf[a][:].rearrange("p (t m j) -> p m j t", t=PACK, j=PACK)[:, m0:m1]
-            src = raw.rearrange("p j (m t) -> p m j t", t=PACK)[:, m0 - raw_m0 : m1 - raw_m0]
-            return dst, src
-
+        gather(0, 0)
+        gather(0, 1)
+        w3_codes = sb("w3_codes", [P, PASSES, N], I32, tag="tab0")
+        nc.sync.dma_start(out=w3_codes[:], in_=w3_words.rearrange("a p c i -> p a (c i)").bitcast(I32))
         gather(1, 0)
-        for t in range(PACK):
-            peer_pass(peer0[t], 1, 0, t)
         gather(1, 1)
-        w4_raw = sb("w4_raw", [P, PACK, N], F32, tag="warm")
-        nc.sync.dma_start(out=w4_raw[:], in_=w4.rearrange("(p j) n -> p j n", j=PACK))
+
+        peer = {}
         for t in range(PACK):
-            peer_pass(peer1[t], 1, 1, t)
-        nc.scalar.copy(*w1_views(0, w1_raw0[:], 0, P, 0))
-        nc.vector.tensor_copy(*w1_views(1, w1_raw1[0], 0, 64, 0))
-        nc.vector.tensor_copy(*w1_views(1, w1_raw1[1], 64, P, 64))
-        nc.vector.quantize_mx(out=w1_codes[0][:].bitcast(FP8X4), scales=w1_sc[0][:], in_=w1_bf[0][:])
-        th[0] = placed("th0", [P, PACK, HALF], F32, 0)
-        th[1] = placed("th1", [P, PACK, HALF], F32, 8192)
+            peer[0, t] = bank(t)
+        for a in range(PASSES):
+            for t in range(PACK):
+                peer_pass(peer[0, t], a, 0, t)
         for t in range(PACK):
-            tanh(peer0[t], 0, t)
+            peer[1, t] = bank(4 + t)
+            for a in (1, 0):
+                peer_pass(peer[1, t], a, 1, t)
 
-        def act_pass(acc, a, hf, t):
-            nc.tensor.matmul_mx(
-                out=acc[:],
-                lhsT=w1_codes[a][:, P * t : P * (t + 1)].bitcast(FP8X4),
-                lhsT_scale=w1_sc[a][:, P * t : P * (t + 1)],
-                rhs=v[a, hf].bitcast(FP8X4),
-                rhs_scale=v_plane(a, hf, False),
-                start=(a == 0),
-                stop=(a == PASSES - 1),
-            )
+        w1_bf = {}
+        w1_q = {}
 
-        act0 = [bank(t) for t in range(PACK)]
-        for c0, c1 in ((0, P), (P, 2 * P), (2 * P, H)):
-            nc.vector.quantize_mx(
-                out=w1_codes[1][:, c0:c1].bitcast(FP8X4), scales=w1_sc[1][:, c0:c1], in_=w1_bf[1][:, PACK * c0 : PACK * c1]
-            )
-        for t in range(PACK):
-            for a in range(PASSES):
-                act_pass(act0[t], a, 0, t)
-        for t in range(PACK):
-            tanh(peer1[t], 1, t)
-
-        h = [sb("h%d" % hf, [P, PACK, HALF], F32) for hf in range(HALVES)]
-        h_rows = out_1.rearrange("(p t) j -> p t j", t=PACK)
-
-        def subtract(acc, hf, t):
-            nc.vector.scalar_tensor_tensor(h[hf][:, t, :], th[hf][:, t, :], neg_gain[:, t : t + 1], acc[:], MULT, ADD)
-            nc.sync.dma_start(out=h_rows[:, t, HALF * hf : HALF * (hf + 1)], in_=h[hf][:, t, :])
-
-        for t in range(PACK):
-            subtract(act0[t], 0, t)
-
-        w4_bf = sb("w4_bf", [P, PACK * N], BF16)
-        w4_codes = sb("w4_codes", [P, N], U32)
-        w4_sc = sb("w4_sc", [P, N], U8)
-        w4_dst = w4_bf[:].rearrange("p (c i j) -> p c j i", i=4, j=PACK)
-        w4_src = w4_raw[:].rearrange("p j (c i) -> p c j i", i=4)
-        nc.scalar.copy(w4_dst[:, 0:64], w4_src[:, 0:64])
-
-        act1 = [bank(4 + t) for t in range(PACK)]
-        for t in range(PACK):
-            for a in range(PASSES):
-                act_pass(act1[t], a, 1, t)
-
-        h_bf = [sb("h_bf%d" % hf, [P, PACK * HALF], BF16) for hf in range(HALVES)]
-        h_codes = [sb("h_codes%d" % hf, [P, HALF], U32) for hf in range(HALVES)]
-        h_sc = sb("h_sc", [P, S], U8)
-
-        def h_views(c):
-            hf, u = divmod(c, 2)
-            dst = h_bf[hf][:, PACK * QUARTER * u : PACK * QUARTER * (u + 1)].rearrange("p (c i t) -> p c t i", i=4, t=PACK)
-            src = h[hf][:, :, QUARTER * u : QUARTER * (u + 1)].rearrange("p t (c i) -> p c t i", i=4)
+        def w1_views(a, t0, t1):
+            w1_bf[a, t0] = sb("w1_bf%d%d" % (a, t0), [P, (t1 - t0) * H], BF16)
+            dst = w1_bf[a, t0][:].rearrange("p (t m j) -> p m j t", t=t1 - t0, j=PACK)
+            src = w1_raw[a][:].rearrange("p j (m t) -> p m j t", t=PACK)[:, :, :, t0:t1]
             return dst, src
 
-        def h_quantize(hf):
-            nc.vector.quantize_mx(
-                out=h_codes[hf][:].bitcast(FP8X4),
-                scales=h_sc[:, HALF * hf : HALF * (hf + 1)],
-                in_=h_bf[hf][:],
-            )
-
-        for c in (0, 1):
-            nc.scalar.copy(*h_views(c))
-        for t in range(PACK):
-            subtract(act1[t], 1, t)
+        def w1_quantize(a, t0, t1, tag=None):
+            width = P * (t1 - t0)
+            codes = sb("w1_codes%d%d" % (a, t0), [P, width], U32, tag=tag)
+            scales = sb("w1_sc%d%d" % (a, t0), [P, width], U8)
+            nc.vector.quantize_mx(out=codes[:].bitcast(FP8X4), scales=scales[:], in_=w1_bf[a, t0][:])
+            for t in range(t0, t1):
+                cols = slice(P * (t - t0), P * (t - t0 + 1))
+                w1_q[a, t] = (codes[:, cols].bitcast(FP8X4), scales[:, cols])
 
         direct = {}
 
-        def direct_tile(b, hf, n):
-            if n == 0:
-                direct[hf] = sb("direct%d" % hf, [P, N_TILES, HALF], F32, tag="h%d" % hf)
+        def direct_tile(b, hf, n, out=None):
             acc = bank(b)
             for a in range(PASSES):
-                nc.tensor.matmul_mx(
-                    out=acc[:],
-                    lhsT=w3_codes[:, a, P * n : P * (n + 1)].bitcast(FP8X4),
-                    lhsT_scale=w3_sc[:, a, P * n : P * (n + 1)],
-                    rhs=v[a, hf].bitcast(FP8X4),
-                    rhs_scale=v_plane(a, hf, False),
-                    start=(a == 0),
-                    stop=(a == PASSES - 1),
+                first_stage(
+                    acc, w3_codes[:, a, P * n : P * (n + 1)].bitcast(FP8X4), w3_sc[8 + 4 * a :, P * n : P * (n + 1)], a, hf
                 )
-            nc.scalar.copy(direct[hf][:, n, :], acc[:])
+            direct[hf, n] = sb("direct%d%d" % (hf, n), [P, HALF], F32)[:] if out is None else out
+            nc.scalar.copy(direct[hf, n], acc[:])
+
+        th = {}
+
+        def tanh(hf, t):
+            nc.scalar.activation(th[hf, t], peer[hf, t][:], TANH, bias=bt_sb[:, t : t + 1])
+
+        def act_sum(b, hf, t, first):
+            act[hf, t] = bank(b)
+            for a in (first, 1 - first):
+                first_stage(act[hf, t], w1_q[a, t][0], w1_q[a, t][1], a, hf, first)
+
+        h = [sb("h%d" % hf, [P, PACK, HALF], F32) for hf in range(HALVES)]
+        h_rows = out_1.rearrange("(p t) j -> p t j", t=PACK)
+        act = {}
+
+        def subtract(hf, t):
+            nc.vector.scalar_tensor_tensor(h[hf][:, t, :], th[hf, t], neg_gain[:, t : t + 1], act[hf, t][:], MULT, ADD)
+            nc.sync.dma_start(out=h_rows[:, t, HALF * hf : HALF * (hf + 1)], in_=h[hf][:, t, :])
+
+        h_bf = [sb("h_bf%d" % hf, [P, PACK * HALF], BF16) for hf in range(HALVES)]
+        h_codes = {}
+        h_sc = sb("h_sc", [P, S], U8)
+        code_rows = out_2[0].rearrange("p m t -> p (m t)").bitcast(I32)
+
+        def h_views(hf, c0, c1):
+            dst = h_bf[hf][:, PACK * c0 : PACK * c1].rearrange("p (c i t) -> p c t i", i=4, t=PACK)
+            src = h[hf][:, :, c0:c1].rearrange("p t (c i) -> p c t i", i=4)
+            return dst, src
+
+        def h_quantize(hf, tag=None):
+            h_codes[hf] = sb("h_codes%d" % hf, [P, HALF], U32, tag=tag)
+            nc.vector.quantize_mx(
+                out=h_codes[hf][:].bitcast(FP8X4), scales=h_sc[:, HALF * hf : HALF * (hf + 1)], in_=h_bf[hf][:]
+            )
+            nc.sync.dma_start(out=code_rows[:, HALF * hf : HALF * (hf + 1)], in_=h_codes[hf][:].bitcast(I32))
+
+        w4_sc = sb("w4_sc", [P, N], U8)
 
         def ring_tile(b, hf, n):
             acc = bank(b)
@@ -281,33 +222,57 @@ def tile_list_fraud_ring_cards_kernel(
                 start=True,
                 stop=True,
             )
-            y = sb("y%d%d" % (hf, n), [P, HALF], F32)
-            nc.vector.tensor_tensor(y[:], acc[:], direct[hf][:, n, :], MULT)
-            nc.sync.dma_start(out=out_0[P * n : P * (n + 1), HALF * hf : HALF * (hf + 1)], in_=y[:])
+            width = QUARTER if (hf, n) == (HALVES - 1, N_TILES - 1) else HALF
+            for c in range(0, HALF, width):
+                y = sb("y%d%d%d" % (hf, n, c), [P, width], F32)
+                nc.vector.tensor_tensor(y[:], acc[:, c : c + width], direct[hf, n][:, c : c + width], MULT)
+                nc.sync.dma_start(out=out_0[P * n : P * (n + 1), HALF * hf + c : HALF * hf + c + width], in_=y[:])
 
-        code_rows = out_2[0].rearrange("p m t -> p (m t)").bitcast(I32)
+        for t in range(PACK):
+            th[0, t] = sb("th0%d" % t, [P, HALF], F32)[:]
+            tanh(0, t)
+        nc.vector.tensor_copy(*w1_views(0, 0, 4))
+        w4_raw = sb("w4_raw", [P, PACK, N], F32, tag="tab_sc")
+        nc.sync.dma_start(out=w4_raw[:], in_=w4.rearrange("(p j) n -> p j n", j=PACK))
+        w1_quantize(0, 0, 4)
+        nc.vector.tensor_copy(*w1_views(1, 0, 2))
+        w1_quantize(1, 0, 2)
+        nc.vector.tensor_copy(*w1_views(1, 2, 4))
+        for t in range(PACK):
+            th[1, t] = sb("th1%d" % t, [P, HALF], F32)[:]
+            tanh(1, t)
+        for t in range(PACK):
+            if t == 1:
+                w1_quantize(1, 2, 4)
+            act_sum(t, 0, t, t % 2)
+            subtract(0, t)
+        w4_bf = sb("w4_bf", [P, PACK * N], BF16, tag="w1_bf12")
+        nc.gpsimd.tensor_scalar(
+            w4_bf[:].rearrange("p (c i j) -> p c j i", i=4, j=PACK), w4_raw[:].rearrange("p j (c i) -> p c j i", i=4),
+            1.0, 0.0, MULT, ADD,
+        )
+        direct_tile(0, 0, 0)
+        for t in range(PACK):
+            act_sum(4 + t, 1, t, 1)
+            subtract(1, t)
+        nc.scalar.copy(*h_views(0, 0, HALF))
+        nc.scalar.copy(*h_views(1, 0, HALF))
 
-        def store_codes(hf):
-            nc.sync.dma_start(out=code_rows[:, HALF * hf : HALF * (hf + 1)], in_=h_codes[hf][:].bitcast(I32))
-
-        for n in range(N_TILES):
-            direct_tile(n, 0, n)
-        nc.vector.tensor_copy(w4_dst[:, 64:96], w4_src[:, 64:96])
+        h_quantize(0)
+        w4_codes = sb("w4_codes", [P, N], U32, tag="th13")
         for c0, c1 in ((0, 256), (256, N)):
             nc.vector.quantize_mx(
                 out=w4_codes[:, c0:c1].bitcast(FP8X4), scales=w4_sc[:, c0:c1], in_=w4_bf[:, PACK * c0 : PACK * c1]
             )
-        h_quantize(0)
-        store_codes(0)
-        nc.scalar.copy(*h_views(2))
-        nc.vector.tensor_copy(*h_views(3))
-        for n, b in enumerate((3, 0, 1)):
-            ring_tile(b, 0, n)
-        for n in range(N_TILES):
-            direct_tile(4 + n, 1, n)
-        h_quantize(1)
-        store_codes(1)
+        late = sb("late", [P, HALVES * N_TILES - 1, HALF], F32, tag="h_bf0")
+        for i in range(1, HALVES * N_TILES):
+            hf, n = divmod(i, N_TILES)
+            direct_tile(4 * hf + n, hf, n, late[:, i - 1, :])
+        ring_tile(3, 0, 0)
+        h_quantize(1, "direct00")
         for q in range(QUADS):
             nc.sync.dma_start(out=out_3[0][4 * q : 4 * q + 4, :].bitcast(I32), in_=h_sc[32 * q : 32 * q + 4, :].bitcast(I32))
-        for n, b in enumerate((7, 2, 3)):
-            ring_tile(b, 1, n)
+        ring_tile(7, 0, 1)
+        ring_tile(0, 0, 2)
+        for n in range(N_TILES):
+            ring_tile(1 + n, 1, n)

@@ -111,8 +111,8 @@ def tile_list_fraud_ring_cards_kernel(
 
         v = {}
 
-        def gather(a, hf, tag=None):
-            v[a, hf] = sb("v%d%d" % (a, hf), [P, HALF], U32, tag=tag)[:]
+        def gather(a, hf):
+            v[a, hf] = sb("v%d%d" % (a, hf), [P, HALF], U32)[:]
             nc.vector.tensor_copy(v[a, hf], tab[a][:].bitcast(U32).indirect(offsets[:, 32 * hf : 32 * (hf + 1)]))
 
         def v_plane(a, hf):
@@ -129,17 +129,18 @@ def tile_list_fraud_ring_cards_kernel(
 
         gather(0, 0)
         gather(0, 1)
-        w3_codes = sb("w3_codes", [P, PASSES, N], I32, tag="tab0")
-        nc.sync.dma_start(out=w3_codes[:], in_=w3_words.rearrange("a p c i -> p a (c i)").bitcast(I32))
+        w4_raw = sb("w4_raw", [P, PACK, N], F32, tag="tab0")
+        nc.sync.dma_start(out=w4_raw[:], in_=w4.rearrange("(p j) n -> p j n", j=PACK))
         gather(1, 0)
         gather(1, 1)
+        w3_codes = sb("w3_codes", [P, PASSES, N], I32, tag="w2_sc_raw")
+        nc.sync.dma_start(out=w3_codes[:], in_=w3_words.rearrange("a p c i -> p a (c i)").bitcast(I32))
 
         peer = {}
         for t in range(PACK):
             peer[0, t] = bank(t)
-        for a in range(PASSES):
-            for t in range(PACK):
-                peer_pass(peer[0, t], a, 0, t)
+        for a, t in ((0, 0), (0, 1), (0, 2), (1, 0), (1, 1), (0, 3), (1, 2), (1, 3)):
+            peer_pass(peer[0, t], a, 0, t)
         for t in range(PACK):
             peer[1, t] = bank(4 + t)
             for a in (1, 0):
@@ -232,8 +233,6 @@ def tile_list_fraud_ring_cards_kernel(
             th[0, t] = sb("th0%d" % t, [P, HALF], F32)[:]
             tanh(0, t)
         nc.vector.tensor_copy(*w1_views(0, 0, 4))
-        w4_raw = sb("w4_raw", [P, PACK, N], F32, tag="tab_sc")
-        nc.sync.dma_start(out=w4_raw[:], in_=w4.rearrange("(p j) n -> p j n", j=PACK))
         w1_quantize(0, 0, 4)
         nc.vector.tensor_copy(*w1_views(1, 0, 2))
         w1_quantize(1, 0, 2)
@@ -241,18 +240,18 @@ def tile_list_fraud_ring_cards_kernel(
         for t in range(PACK):
             th[1, t] = sb("th1%d" % t, [P, HALF], F32)[:]
             tanh(1, t)
+        w4_bf = sb("w4_bf", [P, PACK * N], BF16)
+        nc.scalar.copy(
+            w4_bf[:].rearrange("p (c i j) -> p c j i", i=4, j=PACK), w4_raw[:].rearrange("p j (c i) -> p c j i", i=4)
+        )
         for t in range(PACK):
             if t == 1:
                 w1_quantize(1, 2, 4)
             act_sum(t, 0, t, t % 2)
             subtract(0, t)
-        w4_bf = sb("w4_bf", [P, PACK * N], BF16, tag="w1_bf12")
-        nc.gpsimd.tensor_scalar(
-            w4_bf[:].rearrange("p (c i j) -> p c j i", i=4, j=PACK), w4_raw[:].rearrange("p j (c i) -> p c j i", i=4),
-            1.0, 0.0, MULT, ADD,
-        )
-        direct_tile(0, 0, 0)
         for t in range(PACK):
+            if t == 0:
+                direct_tile(0, 0, 0)
             act_sum(4 + t, 1, t, 1)
             subtract(1, t)
         nc.scalar.copy(*h_views(0, 0, HALF))

@@ -70,12 +70,10 @@ def tile_list_fraud_ring_cards_kernel(
             tab.append(words)
 
         load_table(0, None)
-        gain_sb = sb("gain_sb", [P, PACK], F32)
-        nc.sync.dma_start(out=gain_sb[:], in_=gain.rearrange("(p t) -> p t", t=PACK))
         bt_sb = sb("bt_sb", [P, PACK], F32)
         nc.sync.dma_start(out=bt_sb[:], in_=bt.rearrange("(p t) -> p t", t=PACK))
-        neg_gain = sb("neg_gain", [P, PACK], F32)
-        nc.scalar.mul(neg_gain[:], gain_sb[:], -1.0)
+        neg_bt = sb("neg_bt", [P, PACK], F32)
+        nc.scalar.mul(neg_bt[:], bt_sb[:], -1.0)
 
         w2_sc_dealt = sb("w2_sc_dealt", [P, H], U8)
         nc.vector.tensor_copy(
@@ -87,6 +85,11 @@ def tile_list_fraud_ring_cards_kernel(
         nc.vector.tensor_copy(picked_sc[:], tab_sc[:].indirect(offsets[:]))
         move_to_planes(nc.sync, v_sc, picked_sc)
 
+        for i in range(4):
+            nc.tensor.matmul_mx(
+                out=bank(7)[:], lhsT=w2_raw[:, 0, 0:256].bitcast(FP4X4), lhsT_scale=w2_sc[:, 0:P],
+                rhs=tab[0][:, 0:HALF].bitcast(FP8X4), rhs_scale=w2_sc[:, 0:HALF], start=True, stop=True,
+            )
         w2_codes = sb("w2_codes", [P, PASSES, 2 * H], U8)
         nc.vector.tensor_copy(
             w2_codes[:].bitcast(U16).rearrange("p a (t m) -> p a t m", t=PACK),
@@ -100,7 +103,9 @@ def tile_list_fraud_ring_cards_kernel(
             w1_raw.append(raw)
 
         load_w1(0, "tab_sc")
-        load_w1(1, "w2_raw")
+        load_w1(1, "w2_sc_dealt")
+        gain_sb = sb("gain_sb", [P, PACK], F32)
+        nc.sync.dma_start(out=gain_sb[:], in_=gain.rearrange("(p t) -> p t", t=PACK))
         w3_sc = sb("w3_sc", [P, N], U8, tag="picked_sc")
         nc.gpsimd.memset(w3_sc[:].bitcast(I32), 0)
         for q in range(QUADS):
@@ -178,7 +183,7 @@ def tile_list_fraud_ring_cards_kernel(
         th = {}
 
         def tanh(hf, t):
-            nc.scalar.activation(th[hf, t], peer[hf, t][:], TANH, bias=bt_sb[:, t : t + 1])
+            nc.scalar.activation(th[hf, t], peer[hf, t][:], TANH, bias=neg_bt[:, t : t + 1], scale=-1.0)
 
         def act_sum(b, hf, t, first):
             act[hf, t] = bank(b)
@@ -190,7 +195,7 @@ def tile_list_fraud_ring_cards_kernel(
         act = {}
 
         def subtract(hf, t):
-            nc.vector.scalar_tensor_tensor(h[hf][:, t, :], th[hf, t], neg_gain[:, t : t + 1], act[hf, t][:], MULT, ADD)
+            nc.vector.scalar_tensor_tensor(h[hf][:, t, :], th[hf, t], gain_sb[:, t : t + 1], act[hf, t][:], MULT, ADD)
             nc.sync.dma_start(out=h_rows[:, t, HALF * hf : HALF * (hf + 1)], in_=h[hf][:, t, :])
 
         h_bf = [sb("h_bf%d" % hf, [P, PACK * HALF], BF16) for hf in range(HALVES)]
@@ -210,14 +215,25 @@ def tile_list_fraud_ring_cards_kernel(
             )
             nc.sync.dma_start(out=code_rows[:, HALF * hf : HALF * (hf + 1)], in_=h_codes[hf][:].bitcast(I32))
 
-        w4_sc = sb("w4_sc", [P, N], U8)
+        w4_q = {}
+
+        def w4_quantize(n0, n1, tag):
+            width = P * (n1 - n0)
+            codes = sb("w4_codes%d" % n0, [P, width], U32, tag=tag)
+            scales = sb("w4_sc%d" % n0, [P, width], U8)
+            nc.vector.quantize_mx(
+                out=codes[:].bitcast(FP8X4), scales=scales[:], in_=w4_bf[:, PACK * P * n0 : PACK * P * n1]
+            )
+            for n in range(n0, n1):
+                cols = slice(P * (n - n0), P * (n - n0 + 1))
+                w4_q[n] = (codes[:, cols].bitcast(FP8X4), scales[:, cols])
 
         def ring_tile(b, hf, n):
             acc = bank(b)
             nc.tensor.matmul_mx(
                 out=acc[:],
-                lhsT=w4_codes[:, P * n : P * (n + 1)].bitcast(FP8X4),
-                lhsT_scale=w4_sc[:, P * n : P * (n + 1)],
+                lhsT=w4_q[n][0],
+                lhsT_scale=w4_q[n][1],
                 rhs=h_codes[hf][:].bitcast(FP8X4),
                 rhs_scale=h_sc[:, HALF * hf : HALF * (hf + 1)],
                 start=True,
@@ -229,49 +245,50 @@ def tile_list_fraud_ring_cards_kernel(
                 nc.vector.tensor_tensor(y[:], acc[:, c : c + width], direct[hf, n][:, c : c + width], MULT)
                 nc.sync.dma_start(out=out_0[P * n : P * (n + 1), HALF * hf + c : HALF * hf + c + width], in_=y[:])
 
+        nc.scalar.copy(*w1_views(0, 2, 4))
+        nc.vector.tensor_copy(*w1_views(0, 0, 2))
+        th0 = sb("th0", [P, PACK, HALF], F32, tag="tab_sc")
         for t in range(PACK):
-            th[0, t] = sb("th0%d" % t, [P, HALF], F32)[:]
+            th[0, t] = th0[:, t, :]
             tanh(0, t)
-        nc.vector.tensor_copy(*w1_views(0, 0, 4))
-        w1_quantize(0, 0, 4)
+        w1_quantize(0, 2, 4)
+        w1_quantize(0, 0, 2)
         nc.vector.tensor_copy(*w1_views(1, 0, 2))
-        w1_quantize(1, 0, 2)
         nc.vector.tensor_copy(*w1_views(1, 2, 4))
+        w1_quantize(1, 0, 2)
+        w1_quantize(1, 2, 4)
         for t in range(PACK):
             th[1, t] = sb("th1%d" % t, [P, HALF], F32)[:]
             tanh(1, t)
-        w4_bf = sb("w4_bf", [P, PACK * N], BF16)
-        nc.scalar.copy(
-            w4_bf[:].rearrange("p (c i j) -> p c j i", i=4, j=PACK), w4_raw[:].rearrange("p j (c i) -> p c j i", i=4)
-        )
+        w4_bf = sb("w4_bf", [P, PACK * N], BF16, tag="w1_bf12")
+        for c0, c1 in ((0, P), (P, N)):
+            nc.gpsimd.tensor_scalar(
+                w4_bf[:, PACK * c0 : PACK * c1].rearrange("p (c i j) -> p c j i", i=4, j=PACK),
+                w4_raw[:, :, c0:c1].rearrange("p j (c i) -> p c j i", i=4),
+                1.0, 0.0, MULT, ADD,
+            )
         for t in range(PACK):
-            if t == 1:
-                w1_quantize(1, 2, 4)
-            act_sum(t, 0, t, t % 2)
+            act_sum(t, 0, t, min(t, 1))
             subtract(0, t)
+        direct_tile(0, 0, 0)
         for t in range(PACK):
-            if t == 0:
-                direct_tile(0, 0, 0)
+            if t == PACK - 1:
+                w4_quantize(0, 1, "th11")
             act_sum(4 + t, 1, t, 1)
             subtract(1, t)
         nc.scalar.copy(*h_views(0, 0, HALF))
         nc.scalar.copy(*h_views(1, 0, HALF))
 
         h_quantize(0)
-        w4_codes = sb("w4_codes", [P, N], U32, tag="th13")
-        for c0, c1 in ((0, 256), (256, N)):
-            nc.vector.quantize_mx(
-                out=w4_codes[:, c0:c1].bitcast(FP8X4), scales=w4_sc[:, c0:c1], in_=w4_bf[:, PACK * c0 : PACK * c1]
-            )
-        late = sb("late", [P, HALVES * N_TILES - 1, HALF], F32, tag="h_bf0")
-        for i in range(1, HALVES * N_TILES):
-            hf, n = divmod(i, N_TILES)
-            direct_tile(4 * hf + n, hf, n, late[:, i - 1, :])
+        w4_quantize(1, N_TILES, "th13")
+        late = sb("late", [P, 5, HALF], F32, tag="h_bf0")
+        for i, (b, hf, n) in enumerate(((1, 0, 1), (2, 0, 2), (4, 1, 0), (5, 1, 1), (7, 1, 2))):
+            direct_tile(b, hf, n, late[:, i, :])
         ring_tile(3, 0, 0)
-        h_quantize(1, "direct00")
+        h_quantize(1)
         for q in range(QUADS):
             nc.sync.dma_start(out=out_3[0][4 * q : 4 * q + 4, :].bitcast(I32), in_=h_sc[32 * q : 32 * q + 4, :].bitcast(I32))
-        ring_tile(7, 0, 1)
-        ring_tile(0, 0, 2)
+        ring_tile(0, 0, 1)
+        ring_tile(6, 0, 2)
         for n in range(N_TILES):
-            ring_tile(1 + n, 1, n)
+            ring_tile((3, 1, 0)[n], 1, n)

@@ -75,26 +75,6 @@ def tile_list_fraud_ring_cards_kernel(
         neg_bt = sb("neg_bt", [P, PACK], F32)
         nc.scalar.mul(neg_bt[:], bt_sb[:], -1.0)
 
-        w2_sc_dealt = sb("w2_sc_dealt", [P, H], U8)
-        nc.vector.tensor_copy(
-            w2_sc_dealt[:].rearrange("p (t m) -> p t m", t=PACK), w2_sc_raw[:].rearrange("p (m t) -> p t m", t=PACK)
-        )
-        move_to_planes(nc.sync, w2_sc, w2_sc_dealt)
-        load_table(1, "w2_sc_raw")
-        picked_sc = sb("picked_sc", [P, S], U8)
-        nc.vector.tensor_copy(picked_sc[:], tab_sc[:].indirect(offsets[:]))
-        move_to_planes(nc.sync, v_sc, picked_sc)
-
-        for i in range(4):
-            nc.tensor.matmul_mx(
-                out=bank(7)[:], lhsT=w2_raw[:, 0, 0:256].bitcast(FP4X4), lhsT_scale=w2_sc[:, 0:P],
-                rhs=tab[0][:, 0:HALF].bitcast(FP8X4), rhs_scale=w2_sc[:, 0:HALF], start=True, stop=True,
-            )
-        w2_codes = sb("w2_codes", [P, PASSES, 2 * H], U8)
-        nc.vector.tensor_copy(
-            w2_codes[:].bitcast(U16).rearrange("p a (t m) -> p a t m", t=PACK),
-            w2_raw[:].bitcast(U16).rearrange("p a (m t) -> p a t m", t=PACK),
-        )
         w1_raw = []
 
         def load_w1(a, tag):
@@ -102,9 +82,24 @@ def tile_list_fraud_ring_cards_kernel(
             nc.sync.dma_start(out=raw[:], in_=w1[512 * a : 512 * (a + 1), :].rearrange("(p j) c -> p j c", j=PACK))
             w1_raw.append(raw)
 
-        load_w1(0, "tab_sc")
-        load_w1(1, "w2_sc_dealt")
-        gain_sb = sb("gain_sb", [P, PACK], F32)
+        w2_sc_dealt = sb("w2_sc_dealt", [P, H], U8)
+        nc.vector.tensor_copy(
+            w2_sc_dealt[:].rearrange("p (t m) -> p t m", t=PACK), w2_sc_raw[:].rearrange("p (m t) -> p t m", t=PACK)
+        )
+        move_to_planes(nc.sync, w2_sc, w2_sc_dealt)
+        load_w1(0, "w2_sc_raw")
+        picked_sc = sb("picked_sc", [P, S], U8)
+        nc.vector.tensor_copy(picked_sc[:], tab_sc[:].indirect(offsets[:]))
+        move_to_planes(nc.sync, v_sc, picked_sc)
+
+        w2_codes = sb("w2_codes", [P, PASSES, 2 * H], U8)
+        nc.vector.tensor_copy(
+            w2_codes[:].bitcast(U16).rearrange("p a (t m) -> p a t m", t=PACK),
+            w2_raw[:].bitcast(U16).rearrange("p a (m t) -> p a t m", t=PACK),
+        )
+        load_table(1, "tab_sc")
+        load_w1(1, "w2_raw")
+        gain_sb = sb("gain_sb", [P, PACK], F32, tag="w2_sc_dealt")
         nc.sync.dma_start(out=gain_sb[:], in_=gain.rearrange("(p t) -> p t", t=PACK))
         w3_sc = sb("w3_sc", [P, N], U8, tag="picked_sc")
         nc.gpsimd.memset(w3_sc[:].bitcast(I32), 0)
@@ -130,26 +125,12 @@ def tile_list_fraud_ring_cards_kernel(
             )
 
         def peer_pass(acc, a, hf, t):
-            first_stage(acc, w2_codes[:, a, 256 * t : 256 * (t + 1)].bitcast(FP4X4), w2_sc[:, H * a + P * t : H * a + P * (t + 1)], a, hf, hf)
+            first_stage(acc, w2_codes[:, a, 256 * t : 256 * (t + 1)].bitcast(FP4X4), w2_sc[:, H * a + P * t : H * a + P * (t + 1)], a, hf)
 
         gather(0, 0)
         gather(0, 1)
         w4_raw = sb("w4_raw", [P, PACK, N], F32, tag="tab0")
         nc.sync.dma_start(out=w4_raw[:], in_=w4.rearrange("(p j) n -> p j n", j=PACK))
-        gather(1, 0)
-        gather(1, 1)
-        w3_codes = sb("w3_codes", [P, PASSES, N], I32, tag="w2_sc_raw")
-        nc.sync.dma_start(out=w3_codes[:], in_=w3_words.rearrange("a p c i -> p a (c i)").bitcast(I32))
-
-        peer = {}
-        for t in range(PACK):
-            peer[0, t] = bank(t)
-        for a, t in ((0, 0), (0, 1), (0, 2), (1, 0), (1, 1), (0, 3), (1, 2), (1, 3)):
-            peer_pass(peer[0, t], a, 0, t)
-        for t in range(PACK):
-            peer[1, t] = bank(4 + t)
-            for a in (1, 0):
-                peer_pass(peer[1, t], a, 1, t)
 
         w1_bf = {}
         w1_q = {}
@@ -245,14 +226,24 @@ def tile_list_fraud_ring_cards_kernel(
                 nc.vector.tensor_tensor(y[:], acc[:, c : c + width], direct[hf, n][:, c : c + width], MULT)
                 nc.sync.dma_start(out=out_0[P * n : P * (n + 1), HALF * hf + c : HALF * hf + c + width], in_=y[:])
 
-        nc.scalar.copy(*w1_views(0, 2, 4))
-        nc.vector.tensor_copy(*w1_views(0, 0, 2))
-        th0 = sb("th0", [P, PACK, HALF], F32, tag="tab_sc")
-        for t in range(PACK):
-            th[0, t] = th0[:, t, :]
-            tanh(0, t)
-        w1_quantize(0, 2, 4)
+        nc.scalar.copy(*w1_views(0, 0, 2))
+        nc.vector.tensor_copy(*w1_views(0, 2, 4))
         w1_quantize(0, 0, 2)
+        w1_quantize(0, 2, 4)
+        gather(1, 0)
+        gather(1, 1)
+        w3_codes = sb("w3_codes", [P, PASSES, N], I32, tag="tab_sc")
+        nc.sync.dma_start(out=w3_codes[:], in_=w3_words.rearrange("a p c i -> p a (c i)").bitcast(I32))
+        peer = {}
+        for a in range(PASSES):
+            for hf in range(HALVES):
+                for t in range(PACK):
+                    if a == 0:
+                        peer[hf, t] = bank(PACK * hf + t)
+                    peer_pass(peer[hf, t], a, hf, t)
+        for t in range(PACK):
+            th[0, t] = sb("th0%d" % t, [P, HALF], F32)[:]
+            tanh(0, t)
         nc.vector.tensor_copy(*w1_views(1, 0, 2))
         nc.vector.tensor_copy(*w1_views(1, 2, 4))
         w1_quantize(1, 0, 2)
@@ -277,17 +268,18 @@ def tile_list_fraud_ring_cards_kernel(
             act_sum(4 + t, 1, t, 1)
             subtract(1, t)
         nc.scalar.copy(*h_views(0, 0, HALF))
-        nc.scalar.copy(*h_views(1, 0, HALF))
+        nc.scalar.copy(*h_views(1, 0, QUARTER))
+        nc.vector.tensor_copy(*h_views(1, QUARTER, HALF))
 
         h_quantize(0)
         w4_quantize(1, N_TILES, "th13")
         late = sb("late", [P, 5, HALF], F32, tag="h_bf0")
         for i, (b, hf, n) in enumerate(((1, 0, 1), (2, 0, 2), (4, 1, 0), (5, 1, 1), (7, 1, 2))):
             direct_tile(b, hf, n, late[:, i, :])
-        ring_tile(3, 0, 0)
         h_quantize(1)
         for q in range(QUADS):
             nc.sync.dma_start(out=out_3[0][4 * q : 4 * q + 4, :].bitcast(I32), in_=h_sc[32 * q : 32 * q + 4, :].bitcast(I32))
+        ring_tile(3, 0, 0)
         ring_tile(0, 0, 1)
         ring_tile(6, 0, 2)
         for n in range(N_TILES):

@@ -25,6 +25,7 @@ HALVES = S // HALF
 QUARTER = 256
 N_TILES = N // P
 QUADS = 4
+SC = H + S
 
 
 def tile_list_fraud_ring_cards_kernel(
@@ -34,6 +35,7 @@ def tile_list_fraud_ring_cards_kernel(
     nc = tc.nc
     with ExitStack() as ctx:
         keep = ctx.enter_context(tc.tile_pool(name="keep", bufs=1))
+        turns = ctx.enter_context(tc.tile_pool(name="turns", bufs=1))
         psum = ctx.enter_context(tc.psum_pool(name="psum", bufs=1))
 
         def sb(name, shape, dtype, tag=None):
@@ -47,90 +49,94 @@ def tile_list_fraud_ring_cards_kernel(
         tab_sc = sb("tab_sc", [P, T], U8)
         for rows in (w2_sc_raw, tab_sc):
             nc.vector.memset(rows[0:96, :].bitcast(I32), 0)
-        w2_sc = sb("w2_sc", [P, PASSES * H], U8)
-        nc.gpsimd.memset(w2_sc[:].bitcast(I32), 0)
-        v_sc = sb("v_sc", [P, PASSES * S], U8)
-        nc.gpsimd.memset(v_sc[:].bitcast(I32), 0)
+        planes = [sb("planes%d" % a, [P, SC], U8) for a in range(PASSES)]
+        w3_sc = sb("w3_sc", [P, N], U8)
+        for zeroed in planes + [w3_sc]:
+            nc.gpsimd.memset(zeroed[:].bitcast(I32), 0)
 
-        def move_to_planes(queue, planes, rows):
-            for q in range(QUADS):
-                queue.dma_start(out=planes[32 * q : 32 * q + 4, :].bitcast(I32), in_=rows[96 + 8 * q : 104 + 8 * q, :].bitcast(I32))
+        def load_scale_rows(rows, scales):
+            nc.scalar.dma_start(out=rows.bitcast(I32), in_=scales.rearrange("a q c -> (a q) c").bitcast(I32))
 
-        nc.sync.dma_start(out=w2_sc_raw[96:128, :].bitcast(I32), in_=w2_scales.rearrange("a q c -> q a c").bitcast(I32))
+        def move_to_planes(a):
+            for r in range(4):
+                nc.sync.dma_start(
+                    out=planes[a][r:P:32, :].bitcast(I32), in_=sc_rows[96 + 16 * a + r : 112 + 16 * a : 4, :].bitcast(I32)
+                )
 
-        nc.sync.dma_start(out=tab_sc[96:128, :].bitcast(I32), in_=tab_scales.rearrange("a q t -> q a t").bitcast(I32))
+        def load_w1(a):
+            w1_raw.append(turns.tile([P, PACK, H], F32, name="w1_raw%d" % a, offset=4 * PACK * H * a, align_bytes=64))
+            nc.sync.dma_start(out=w1_raw[a][:], in_=w1[512 * a : 512 * (a + 1), :].rearrange("(p j) c -> p j c", j=PACK))
+
+        sc_rows = sb("sc_rows", [P, SC], U8)
         nc.sync.dma_start(offsets[:], offs)
+        load_scale_rows(tab_sc[96:128, :], tab_scales)
+        load_scale_rows(w2_sc_raw[96:128, :], w2_scales)
         w2_raw = sb("w2_raw", [P, PASSES, 2 * H], U8)
         nc.sync.dma_start(out=w2_raw[:].bitcast(I32), in_=w2_words.rearrange("a p c -> p a c").bitcast(I32))
         tab = []
-
-        def load_table(a, tag):
-            words = sb("tab%d" % a, [P, T], I32, tag=tag)
-            nc.sync.dma_start(out=words[:], in_=tab_words[a].rearrange("p t i -> p (t i)").bitcast(I32))
-            tab.append(words)
-
-        load_table(0, None)
+        for a in range(PASSES):
+            tab.append(sb("tab%d" % a, [P, T], I32))
+            nc.sync.dma_start(out=tab[a][:], in_=tab_words[a].rearrange("p t i -> p (t i)").bitcast(I32))
         bt_sb = sb("bt_sb", [P, PACK], F32)
         nc.sync.dma_start(out=bt_sb[:], in_=bt.rearrange("(p t) -> p t", t=PACK))
         neg_bt = sb("neg_bt", [P, PACK], F32)
         nc.scalar.mul(neg_bt[:], bt_sb[:], -1.0)
-
-        w1_raw = []
-
-        def load_w1(a, tag):
-            raw = sb("w1_raw%d" % a, [P, PACK, H], F32, tag=tag)
-            nc.sync.dma_start(out=raw[:], in_=w1[512 * a : 512 * (a + 1), :].rearrange("(p j) c -> p j c", j=PACK))
-            w1_raw.append(raw)
-
-        w2_sc_dealt = sb("w2_sc_dealt", [P, H], U8)
-        nc.vector.tensor_copy(
-            w2_sc_dealt[:].rearrange("p (t m) -> p t m", t=PACK), w2_sc_raw[:].rearrange("p (m t) -> p t m", t=PACK)
-        )
-        move_to_planes(nc.sync, w2_sc, w2_sc_dealt)
-        load_w1(0, "w2_sc_raw")
         picked_sc = sb("picked_sc", [P, S], U8)
         nc.vector.tensor_copy(picked_sc[:], tab_sc[:].indirect(offsets[:]))
-        move_to_planes(nc.sync, v_sc, picked_sc)
+        nc.vector.tensor_copy(
+            sc_rows[:, 0:H].rearrange("p (t m) -> p t m", t=PACK), w2_sc_raw[:].rearrange("p (m t) -> p t m", t=PACK)
+        )
+        nc.vector.tensor_copy(sc_rows[96:128, H:SC].bitcast(I32), picked_sc[96:128, :].bitcast(I32))
+        w1_raw = []
+        for a in range(PASSES):
+            move_to_planes(a)
+            load_w1(a)
+        gain_sb = sb("gain_sb", [P, PACK], F32)
+        nc.sync.dma_start(out=gain_sb[:], in_=gain.rearrange("(p t) -> p t", t=PACK))
+        w4_raw = sb("w4_raw", [P, PACK, N], F32)
+        nc.sync.dma_start(out=w4_raw[:], in_=w4.rearrange("(p j) n -> p j n", j=PACK))
+        for q in range(QUADS):
+            nc.sync.dma_start(
+                out=w3_sc[32 * q + 8 : 32 * q + 16, :].bitcast(I32), in_=w3_scales[:, 4 * q : 4 * q + 4, :].bitcast(I32)
+            )
+        w3_codes = sb("w3_codes", [P, PASSES, N], I32)
+        nc.sync.dma_start(out=w3_codes[:], in_=w3_words.rearrange("a p c i -> p a (c i)").bitcast(I32))
 
         w2_codes = sb("w2_codes", [P, PASSES, 2 * H], U8)
         nc.vector.tensor_copy(
             w2_codes[:].bitcast(U16).rearrange("p a (t m) -> p a t m", t=PACK),
             w2_raw[:].bitcast(U16).rearrange("p a (m t) -> p a t m", t=PACK),
         )
-        load_table(1, "tab_sc")
-        load_w1(1, "w2_raw")
-        gain_sb = sb("gain_sb", [P, PACK], F32, tag="w2_sc_dealt")
-        nc.sync.dma_start(out=gain_sb[:], in_=gain.rearrange("(p t) -> p t", t=PACK))
-        w3_sc = sb("w3_sc", [P, N], U8, tag="picked_sc")
-        nc.gpsimd.memset(w3_sc[:].bitcast(I32), 0)
-        for q in range(QUADS):
-            nc.scalar.dma_start(
-                out=w3_sc[32 * q + 8 : 32 * q + 16, :].bitcast(I32),
-                in_=w3_scales[:, 4 * q : 4 * q + 4, :].bitcast(I32),
-            )
 
         v = {}
 
-        def gather(a, hf):
-            v[a, hf] = sb("v%d%d" % (a, hf), [P, HALF], U32)[:]
+        def gather(a, hf, tag=None):
+            v[a, hf] = sb("v%d%d" % (a, hf), [P, HALF], U32, tag=tag)[:]
             nc.vector.tensor_copy(v[a, hf], tab[a][:].bitcast(U32).indirect(offsets[:, 32 * hf : 32 * (hf + 1)]))
 
-        def v_plane(a, hf):
-            return v_sc[:, S * a + HALF * hf : S * a + HALF * (hf + 1)]
+        for a in range(PASSES):
+            for hf in range(HALVES):
+                gather(a, hf)
 
-        def first_stage(acc, codes, scales, a, hf, first=0):
+        def v_plane(a, hf):
+            return planes[a][:, H + HALF * hf : H + HALF * (hf + 1)]
+
+        def first_stage(acc, codes, scales, a, hf, first):
             nc.tensor.matmul_mx(
-                out=acc[:], lhsT=codes, lhsT_scale=scales, rhs=v[a, hf].bitcast(FP8X4), rhs_scale=v_plane(a, hf),
+                out=acc[:], lhsT=codes, lhsT_scale=scales, rhs=v[a, hf].bitcast(FP8X4),
+                rhs_scale=v_plane(a, hf),
                 start=(a == first), stop=(a != first),
             )
 
-        def peer_pass(acc, a, hf, t):
-            first_stage(acc, w2_codes[:, a, 256 * t : 256 * (t + 1)].bitcast(FP4X4), w2_sc[:, H * a + P * t : H * a + P * (t + 1)], a, hf)
+        peer = {}
 
-        gather(0, 0)
-        gather(0, 1)
-        w4_raw = sb("w4_raw", [P, PACK, N], F32, tag="tab0")
-        nc.sync.dma_start(out=w4_raw[:], in_=w4.rearrange("(p j) n -> p j n", j=PACK))
+        def peer_pass(a, hf, t):
+            if a == 0:
+                peer[hf, t] = bank(PACK * hf + t)
+            first_stage(
+                peer[hf, t], w2_codes[:, a, 256 * t : 256 * (t + 1)].bitcast(FP4X4),
+                planes[a][:, P * t : P * (t + 1)], a, hf, 0,
+            )
 
         w1_bf = {}
         w1_q = {}
@@ -141,9 +147,9 @@ def tile_list_fraud_ring_cards_kernel(
             src = w1_raw[a][:].rearrange("p j (m t) -> p m j t", t=PACK)[:, :, :, t0:t1]
             return dst, src
 
-        def w1_quantize(a, t0, t1, tag=None):
+        def w1_quantize(a, t0, t1):
             width = P * (t1 - t0)
-            codes = sb("w1_codes%d%d" % (a, t0), [P, width], U32, tag=tag)
+            codes = sb("w1_codes%d%d" % (a, t0), [P, width], U32)
             scales = sb("w1_sc%d%d" % (a, t0), [P, width], U8)
             nc.vector.quantize_mx(out=codes[:].bitcast(FP8X4), scales=scales[:], in_=w1_bf[a, t0][:])
             for t in range(t0, t1):
@@ -152,19 +158,23 @@ def tile_list_fraud_ring_cards_kernel(
 
         direct = {}
 
-        def direct_tile(b, hf, n, out=None):
+        def direct_tile(b, hf, n):
             acc = bank(b)
             for a in range(PASSES):
                 first_stage(
-                    acc, w3_codes[:, a, P * n : P * (n + 1)].bitcast(FP8X4), w3_sc[8 + 4 * a :, P * n : P * (n + 1)], a, hf
+                    acc, w3_codes[:, a, P * n : P * (n + 1)].bitcast(FP8X4),
+                    w3_sc[8 + 4 * a :, P * n : P * (n + 1)], a, hf, 0,
                 )
-            direct[hf, n] = sb("direct%d%d" % (hf, n), [P, HALF], F32)[:] if out is None else out
+            direct[hf, n] = sb("direct%d%d" % (hf, n), [P, HALF], F32)[:]
             nc.scalar.copy(direct[hf, n], acc[:])
 
         th = {}
 
-        def tanh(hf, t):
-            nc.scalar.activation(th[hf, t], peer[hf, t][:], TANH, bias=neg_bt[:, t : t + 1], scale=-1.0)
+        def tanh(hf, t, out):
+            th[hf, t] = out
+            nc.scalar.activation(out, peer[hf, t][:], TANH, bias=neg_bt[:, t : t + 1], scale=-1.0)
+
+        act = {}
 
         def act_sum(b, hf, t, first):
             act[hf, t] = bank(b)
@@ -173,7 +183,6 @@ def tile_list_fraud_ring_cards_kernel(
 
         h = [sb("h%d" % hf, [P, PACK, HALF], F32) for hf in range(HALVES)]
         h_rows = out_1.rearrange("(p t) j -> p t j", t=PACK)
-        act = {}
 
         def subtract(hf, t):
             nc.vector.scalar_tensor_tensor(h[hf][:, t, :], th[hf, t], gain_sb[:, t : t + 1], act[hf, t][:], MULT, ADD)
@@ -189,32 +198,25 @@ def tile_list_fraud_ring_cards_kernel(
             src = h[hf][:, :, c0:c1].rearrange("p t (c i) -> p c t i", i=4)
             return dst, src
 
-        def h_quantize(hf, tag=None):
-            h_codes[hf] = sb("h_codes%d" % hf, [P, HALF], U32, tag=tag)
+        def h_quantize(hf):
+            h_codes[hf] = sb("h_codes%d" % hf, [P, HALF], U32)
             nc.vector.quantize_mx(
                 out=h_codes[hf][:].bitcast(FP8X4), scales=h_sc[:, HALF * hf : HALF * (hf + 1)], in_=h_bf[hf][:]
             )
             nc.sync.dma_start(out=code_rows[:, HALF * hf : HALF * (hf + 1)], in_=h_codes[hf][:].bitcast(I32))
 
-        w4_q = {}
-
-        def w4_quantize(n0, n1, tag):
-            width = P * (n1 - n0)
-            codes = sb("w4_codes%d" % n0, [P, width], U32, tag=tag)
-            scales = sb("w4_sc%d" % n0, [P, width], U8)
+        def w4_quantize(n0, n1):
+            cols = slice(P * n0, P * n1)
             nc.vector.quantize_mx(
-                out=codes[:].bitcast(FP8X4), scales=scales[:], in_=w4_bf[:, PACK * P * n0 : PACK * P * n1]
+                out=w4_codes[:, cols].bitcast(FP8X4), scales=w4_sc[:, cols], in_=w4_bf[:, PACK * P * n0 : PACK * P * n1]
             )
-            for n in range(n0, n1):
-                cols = slice(P * (n - n0), P * (n - n0 + 1))
-                w4_q[n] = (codes[:, cols].bitcast(FP8X4), scales[:, cols])
 
         def ring_tile(b, hf, n):
             acc = bank(b)
             nc.tensor.matmul_mx(
                 out=acc[:],
-                lhsT=w4_q[n][0],
-                lhsT_scale=w4_q[n][1],
+                lhsT=w4_codes[:, P * n : P * (n + 1)].bitcast(FP8X4),
+                lhsT_scale=w4_sc[:, P * n : P * (n + 1)],
                 rhs=h_codes[hf][:].bitcast(FP8X4),
                 rhs_scale=h_sc[:, HALF * hf : HALF * (hf + 1)],
                 start=True,
@@ -226,61 +228,54 @@ def tile_list_fraud_ring_cards_kernel(
                 nc.vector.tensor_tensor(y[:], acc[:, c : c + width], direct[hf, n][:, c : c + width], MULT)
                 nc.sync.dma_start(out=out_0[P * n : P * (n + 1), HALF * hf + c : HALF * hf + c + width], in_=y[:])
 
-        nc.scalar.copy(*w1_views(0, 0, 2))
-        nc.vector.tensor_copy(*w1_views(0, 2, 4))
-        w1_quantize(0, 0, 2)
-        w1_quantize(0, 2, 4)
-        gather(1, 0)
-        gather(1, 1)
-        w3_codes = sb("w3_codes", [P, PASSES, N], I32, tag="tab_sc")
-        nc.sync.dma_start(out=w3_codes[:], in_=w3_words.rearrange("a p c i -> p a (c i)").bitcast(I32))
-        peer = {}
         for a in range(PASSES):
             for hf in range(HALVES):
                 for t in range(PACK):
-                    if a == 0:
-                        peer[hf, t] = bank(PACK * hf + t)
-                    peer_pass(peer[hf, t], a, hf, t)
+                    peer_pass(a, hf, t)
+        nc.vector.tensor_copy(*w1_views(0, 0, 2))
+        nc.scalar.copy(*w1_views(0, 2, 4))
+        w1_quantize(0, 0, 2)
+        w1_quantize(0, 2, 4)
         for t in range(PACK):
-            th[0, t] = sb("th0%d" % t, [P, HALF], F32)[:]
-            tanh(0, t)
+            tanh(0, t, turns.tile([P, HALF], F32, name="th0%d" % t, offset=4 * H * t, align_bytes=64)[:])
         nc.vector.tensor_copy(*w1_views(1, 0, 2))
         nc.vector.tensor_copy(*w1_views(1, 2, 4))
         w1_quantize(1, 0, 2)
         w1_quantize(1, 2, 4)
         for t in range(PACK):
-            th[1, t] = sb("th1%d" % t, [P, HALF], F32)[:]
-            tanh(1, t)
+            tanh(1, t, sb("th1%d" % t, [P, HALF], F32)[:])
         w4_bf = sb("w4_bf", [P, PACK * N], BF16, tag="w1_bf12")
-        for c0, c1 in ((0, P), (P, N)):
-            nc.gpsimd.tensor_scalar(
-                w4_bf[:, PACK * c0 : PACK * c1].rearrange("p (c i j) -> p c j i", i=4, j=PACK),
-                w4_raw[:, :, c0:c1].rearrange("p j (c i) -> p c j i", i=4),
-                1.0, 0.0, MULT, ADD,
-            )
+        nc.gpsimd.tensor_scalar(
+            w4_bf[:].rearrange("p (c j) -> p c j", j=PACK),
+            w4_raw[:].rearrange("p j c -> p c j"),
+            1.0, 0.0, MULT, ADD,
+        )
         for t in range(PACK):
-            act_sum(t, 0, t, min(t, 1))
+            act_sum(t, 0, t, t // 2)
             subtract(0, t)
-        direct_tile(0, 0, 0)
-        for t in range(PACK):
-            if t == PACK - 1:
-                w4_quantize(0, 1, "th11")
+        nc.scalar.copy(*h_views(0, 0, HALF))
+        for t in range(PACK - 1):
             act_sum(4 + t, 1, t, 1)
             subtract(1, t)
-        nc.scalar.copy(*h_views(0, 0, HALF))
+        w4_codes = sb("w4_codes", [P, N], U32, tag="th11")
+        w4_sc = sb("w4_sc", [P, N], U8)
+        w4_quantize(0, 1)
+        w4_quantize(1, N_TILES)
+        act_sum(7, 1, 3, 1)
+        subtract(1, 3)
+        direct_tile(0, 0, 0)
         nc.scalar.copy(*h_views(1, 0, QUARTER))
-        nc.vector.tensor_copy(*h_views(1, QUARTER, HALF))
-
+        direct_tile(1, 0, 1)
+        direct_tile(2, 0, 2)
         h_quantize(0)
-        w4_quantize(1, N_TILES, "th13")
-        late = sb("late", [P, 5, HALF], F32, tag="h_bf0")
-        for i, (b, hf, n) in enumerate(((1, 0, 1), (2, 0, 2), (4, 1, 0), (5, 1, 1), (7, 1, 2))):
-            direct_tile(b, hf, n, late[:, i, :])
+        nc.vector.tensor_copy(*h_views(1, QUARTER, HALF))
+        ring_tile(3, 0, 0)
         h_quantize(1)
         for q in range(QUADS):
             nc.sync.dma_start(out=out_3[0][4 * q : 4 * q + 4, :].bitcast(I32), in_=h_sc[32 * q : 32 * q + 4, :].bitcast(I32))
-        ring_tile(3, 0, 0)
-        ring_tile(0, 0, 1)
-        ring_tile(6, 0, 2)
+        ring_tile(4, 0, 1)
+        ring_tile(5, 0, 2)
         for n in range(N_TILES):
-            ring_tile((3, 1, 0)[n], 1, n)
+            direct_tile((6, 7, 0)[n], 1, n)
+        for n in range(N_TILES):
+            ring_tile(1 + n, 1, n)

@@ -22,9 +22,10 @@ PACK = 4
 PASSES = K // (P * PACK)
 HALF = 512
 HALVES = S // HALF
-QUARTER = 256
 N_TILES = N // P
 QUADS = 4
+H_SPLIT = 288
+QUARTER = 256
 SC = H + S
 
 
@@ -198,6 +199,14 @@ def tile_list_fraud_ring_cards_kernel(
             src = h[hf][:, :, c0:c1].rearrange("p t (c i) -> p c t i", i=4)
             return dst, src
 
+        def h_cast(hf):
+            nc.scalar.copy(*h_views(hf, 0, H_SPLIT))
+            nc.gpsimd.tensor_scalar(
+                h_bf[hf][:, PACK * H_SPLIT :].rearrange("p (c t) -> p c t", t=PACK),
+                h[hf][:, :, H_SPLIT:].rearrange("p t c -> p c t"),
+                1.0, 0.0, MULT, ADD,
+            )
+
         def h_quantize(hf):
             h_codes[hf] = sb("h_codes%d" % hf, [P, HALF], U32)
             nc.vector.quantize_mx(
@@ -253,29 +262,30 @@ def tile_list_fraud_ring_cards_kernel(
         for t in range(PACK):
             act_sum(t, 0, t, t // 2)
             subtract(0, t)
-        nc.scalar.copy(*h_views(0, 0, HALF))
+        h_cast(0)
         for t in range(PACK - 1):
             act_sum(4 + t, 1, t, 1)
             subtract(1, t)
+        direct_tile(7, 0, 0)
+        direct_tile(0, 0, 1)
         w4_codes = sb("w4_codes", [P, N], U32, tag="th11")
         w4_sc = sb("w4_sc", [P, N], U8)
         w4_quantize(0, 1)
         w4_quantize(1, N_TILES)
-        act_sum(7, 1, 3, 1)
-        subtract(1, 3)
-        direct_tile(0, 0, 0)
-        nc.scalar.copy(*h_views(1, 0, QUARTER))
-        direct_tile(1, 0, 1)
-        direct_tile(2, 0, 2)
         h_quantize(0)
-        nc.vector.tensor_copy(*h_views(1, QUARTER, HALF))
-        ring_tile(3, 0, 0)
+        act_sum(6, 1, 3, 1)
+        subtract(1, 3)
+        h_cast(1)
+        for n in range(2):
+            ring_tile(2 + n, 0, n)
+        direct_tile(1, 0, 2)
         h_quantize(1)
-        for q in range(QUADS):
-            nc.sync.dma_start(out=out_3[0][4 * q : 4 * q + 4, :].bitcast(I32), in_=h_sc[32 * q : 32 * q + 4, :].bitcast(I32))
-        ring_tile(4, 0, 1)
-        ring_tile(5, 0, 2)
-        for n in range(N_TILES):
-            direct_tile((6, 7, 0)[n], 1, n)
-        for n in range(N_TILES):
-            ring_tile(1 + n, 1, n)
+        for r in range(4):
+            nc.sync.dma_start(out=out_3[0][r:16:4, :].bitcast(I32), in_=h_sc[r:P:32, :].bitcast(I32))
+        ring_tile(4, 0, 2)
+        direct_tile(5, 1, 0)
+        direct_tile(7, 1, 1)
+        ring_tile(0, 1, 0)
+        direct_tile(6, 1, 2)
+        ring_tile(1, 1, 1)
+        ring_tile(2, 1, 2)

@@ -56,7 +56,7 @@ def tile_list_fraud_ring_cards_kernel(
             nc.gpsimd.memset(zeroed[:].bitcast(I32), 0)
 
         def load_scale_rows(rows, scales):
-            nc.scalar.dma_start(out=rows.bitcast(I32), in_=scales.rearrange("a q c -> (a q) c").bitcast(I32))
+            nc.sync.dma_start(out=rows.bitcast(I32), in_=scales.rearrange("a q c -> (a q) c").bitcast(I32))
 
         def move_to_planes(a):
             for r in range(4):
@@ -69,8 +69,8 @@ def tile_list_fraud_ring_cards_kernel(
             nc.sync.dma_start(out=w1_raw[a][:], in_=w1[512 * a : 512 * (a + 1), :].rearrange("(p j) c -> p j c", j=PACK))
 
         sc_rows = sb("sc_rows", [P, SC], U8)
-        nc.sync.dma_start(offsets[:], offs)
         load_scale_rows(tab_sc[96:128, :], tab_scales)
+        nc.sync.dma_start(offsets[:], offs)
         load_scale_rows(w2_sc_raw[96:128, :], w2_scales)
         w2_raw = sb("w2_raw", [P, PASSES, 2 * H], U8)
         nc.sync.dma_start(out=w2_raw[:].bitcast(I32), in_=w2_words.rearrange("a p c -> p a c").bitcast(I32))

@@ -20,13 +20,14 @@ TANH = mybir.ActivationFunctionType.Tanh
 P = 128
 PACK = 4
 PASSES = K // (P * PACK)
-HALF = 512
-HALVES = S // HALF
+HALF = S // 2
 N_TILES = N // P
-QUADS = 4
-H_SPLIT = 288
-QUARTER = 256
+ROWS_AT = 96
 SC = H + S
+H_SPLIT = 288
+LAST_PIECE = 256
+SLOT = 4 * HALF
+EARLY_TANH = 3
 
 
 def tile_list_fraud_ring_cards_kernel(
@@ -42,242 +43,220 @@ def tile_list_fraud_ring_cards_kernel(
         def sb(name, shape, dtype, tag=None):
             return keep.tile(shape, dtype, name=name, tag=tag or name, align_bytes=64)
 
+        def placed(name, shape, dtype, offset):
+            return turns.tile(shape, dtype, name=name, offset=offset, align_bytes=64)
+
         def bank(b):
             return psum.tile([P, HALF], F32, name="bank%d" % b)
 
+        def load(tile, source):
+            nc.sync.dma_start(out=tile, in_=source)
+
+        def load_bytes(tile, source):
+            load(tile.bitcast(I32), source.bitcast(I32))
+
         offsets = keep.tile([P, S // 16], U16, name="offsets")
-        w2_sc_raw = sb("w2_sc_raw", [P, H], U8)
         tab_sc = sb("tab_sc", [P, T], U8)
-        for rows in (w2_sc_raw, tab_sc):
-            nc.vector.memset(rows[0:96, :].bitcast(I32), 0)
+        w2_sc = sb("w2_sc", [P, H], U8)
+        for rows in (tab_sc, w2_sc):
+            nc.vector.memset(rows[0:ROWS_AT, :].bitcast(I32), 0)
         planes = [sb("planes%d" % a, [P, SC], U8) for a in range(PASSES)]
         w3_sc = sb("w3_sc", [P, N], U8)
         for zeroed in planes + [w3_sc]:
             nc.gpsimd.memset(zeroed[:].bitcast(I32), 0)
 
-        def load_scale_rows(rows, scales):
-            nc.sync.dma_start(out=rows.bitcast(I32), in_=scales.rearrange("a q c -> (a q) c").bitcast(I32))
-
-        def move_to_planes(a):
-            for r in range(4):
-                nc.sync.dma_start(
-                    out=planes[a][r:P:32, :].bitcast(I32), in_=sc_rows[96 + 16 * a + r : 112 + 16 * a : 4, :].bitcast(I32)
-                )
-
-        def load_w1(a):
-            w1_raw.append(turns.tile([P, PACK, H], F32, name="w1_raw%d" % a, offset=4 * PACK * H * a, align_bytes=64))
-            nc.sync.dma_start(out=w1_raw[a][:], in_=w1[512 * a : 512 * (a + 1), :].rearrange("(p j) c -> p j c", j=PACK))
-
-        sc_rows = sb("sc_rows", [P, SC], U8)
-        load_scale_rows(tab_sc[96:128, :], tab_scales)
+        load_bytes(tab_sc[ROWS_AT:, :], tab_scales.rearrange("a q c -> (a q) c"))
         nc.sync.dma_start(offsets[:], offs)
-        load_scale_rows(w2_sc_raw[96:128, :], w2_scales)
-        w2_raw = sb("w2_raw", [P, PASSES, 2 * H], U8)
-        nc.sync.dma_start(out=w2_raw[:].bitcast(I32), in_=w2_words.rearrange("a p c -> p a c").bitcast(I32))
-        tab = []
-        for a in range(PASSES):
-            tab.append(sb("tab%d" % a, [P, T], I32))
-            nc.sync.dma_start(out=tab[a][:], in_=tab_words[a].rearrange("p t i -> p (t i)").bitcast(I32))
+        load_bytes(w2_sc[ROWS_AT:, :], w2_scales.rearrange("a q c -> (a q) c"))
         bt_sb = sb("bt_sb", [P, PACK], F32)
-        nc.sync.dma_start(out=bt_sb[:], in_=bt.rearrange("(p t) -> p t", t=PACK))
+        gain_sb = sb("gain_sb", [P, PACK], F32)
+        nc.scalar.dma_start(out=bt_sb[:], in_=bt.rearrange("(p t) -> p t", t=PACK))
+        nc.scalar.dma_start(out=gain_sb[:], in_=gain.rearrange("(p t) -> p t", t=PACK))
         neg_bt = sb("neg_bt", [P, PACK], F32)
         nc.scalar.mul(neg_bt[:], bt_sb[:], -1.0)
+        w2_raw = sb("w2_raw", [P, PASSES, 2 * H], U8)
+        load_bytes(w2_raw[:], w2_words.rearrange("a p c -> p a c"))
+        tab = [sb("tab%d" % a, [P, T], I32) for a in range(PASSES)]
+        for a in range(PASSES):
+            load(tab[a][:], tab_words[a].rearrange("p t i -> p (t i)").bitcast(I32))
+
         picked_sc = sb("picked_sc", [P, S], U8)
         nc.vector.tensor_copy(picked_sc[:], tab_sc[:].indirect(offsets[:]))
+        sc_rows = sb("sc_rows", [P, SC], U8)
         nc.vector.tensor_copy(
-            sc_rows[:, 0:H].rearrange("p (t m) -> p t m", t=PACK), w2_sc_raw[:].rearrange("p (m t) -> p t m", t=PACK)
+            sc_rows[:, 0:H].rearrange("p (t m) -> p t m", t=PACK), w2_sc[:].rearrange("p (m t) -> p t m", t=PACK)
         )
-        nc.vector.tensor_copy(sc_rows[96:128, H:SC].bitcast(I32), picked_sc[96:128, :].bitcast(I32))
-        w1_raw = []
-        for a in range(PASSES):
-            move_to_planes(a)
-            load_w1(a)
-        gain_sb = sb("gain_sb", [P, PACK], F32)
-        nc.sync.dma_start(out=gain_sb[:], in_=gain.rearrange("(p t) -> p t", t=PACK))
+        nc.vector.tensor_copy(sc_rows[ROWS_AT:, H:SC].bitcast(I32), picked_sc[ROWS_AT:, :].bitcast(I32))
+
+        def move_to_planes(a):
+            first_row = ROWS_AT + 16 * a
+            for r in range(4):
+                load_bytes(planes[a][r:P:32, :], sc_rows[first_row + r : first_row + 16 : 4, :])
+
+        w1_rows = w1.rearrange("(a p j) c -> a p j c", a=PASSES, j=PACK)
+        w1_raw = [sb("w1_raw0", [P, PACK, H], F32), placed("w1_raw1", [P, PACK, H], F32, 0)]
+        move_to_planes(0)
+        load(w1_raw[0][:, 0:2, :], w1_rows[0][:, 0:2, :])
+        move_to_planes(1)
+        load(w1_raw[0][:, 2:4, :], w1_rows[0][:, 2:4, :])
+        load(w1_raw[1][:], w1_rows[1])
         w4_raw = sb("w4_raw", [P, PACK, N], F32)
-        nc.sync.dma_start(out=w4_raw[:], in_=w4.rearrange("(p j) n -> p j n", j=PACK))
-        for q in range(QUADS):
-            nc.sync.dma_start(
-                out=w3_sc[32 * q + 8 : 32 * q + 16, :].bitcast(I32), in_=w3_scales[:, 4 * q : 4 * q + 4, :].bitcast(I32)
-            )
+        load(w4_raw[:], w4.rearrange("(p j) n -> p j n", j=PACK))
+        for q in range(4):
+            load_bytes(w3_sc[32 * q + 8 : 32 * q + 16, :], w3_scales[:, 4 * q : 4 * q + 4, :])
         w3_codes = sb("w3_codes", [P, PASSES, N], I32)
-        nc.sync.dma_start(out=w3_codes[:], in_=w3_words.rearrange("a p c i -> p a (c i)").bitcast(I32))
+        load(w3_codes[:], w3_words.rearrange("a p c i -> p a (c i)").bitcast(I32))
+
+        v = {}
+
+        def gather(a, hf):
+            v[a, hf] = sb("v%d%d" % (a, hf), [P, HALF], U32)[:]
+            nc.vector.tensor_copy(v[a, hf], tab[a][:].bitcast(U32).indirect(offsets[:, 32 * hf : 32 * (hf + 1)]))
 
         w2_codes = sb("w2_codes", [P, PASSES, 2 * H], U8)
         nc.vector.tensor_copy(
             w2_codes[:].bitcast(U16).rearrange("p a (t m) -> p a t m", t=PACK),
             w2_raw[:].bitcast(U16).rearrange("p a (m t) -> p a t m", t=PACK),
         )
-
-        v = {}
-
-        def gather(a, hf, tag=None):
-            v[a, hf] = sb("v%d%d" % (a, hf), [P, HALF], U32, tag=tag)[:]
-            nc.vector.tensor_copy(v[a, hf], tab[a][:].bitcast(U32).indirect(offsets[:, 32 * hf : 32 * (hf + 1)]))
-
         for a in range(PASSES):
-            for hf in range(HALVES):
+            for hf in range(2):
                 gather(a, hf)
-
-        def v_plane(a, hf):
-            return planes[a][:, H + HALF * hf : H + HALF * (hf + 1)]
 
         def first_stage(acc, codes, scales, a, hf, first):
             nc.tensor.matmul_mx(
                 out=acc[:], lhsT=codes, lhsT_scale=scales, rhs=v[a, hf].bitcast(FP8X4),
-                rhs_scale=v_plane(a, hf),
-                start=(a == first), stop=(a != first),
+                rhs_scale=planes[a][:, H + HALF * hf : H + HALF * (hf + 1)], start=(a == first), stop=(a != first),
             )
 
         peer = {}
 
-        def peer_pass(a, hf, t):
-            if a == 0:
+        def peer_pass(a, hf, t, first):
+            if a == first:
                 peer[hf, t] = bank(PACK * hf + t)
-            first_stage(
-                peer[hf, t], w2_codes[:, a, 256 * t : 256 * (t + 1)].bitcast(FP4X4),
-                planes[a][:, P * t : P * (t + 1)], a, hf, 0,
-            )
+            codes = w2_codes[:, a, 2 * P * t : 2 * P * (t + 1)].bitcast(FP4X4)
+            first_stage(peer[hf, t], codes, planes[a][:, P * t : P * (t + 1)], a, hf, first)
 
         w1_bf = {}
         w1_q = {}
 
-        def w1_views(a, t0, t1):
-            w1_bf[a, t0] = sb("w1_bf%d%d" % (a, t0), [P, (t1 - t0) * H], BF16)
-            dst = w1_bf[a, t0][:].rearrange("p (t m j) -> p m j t", t=t1 - t0, j=PACK)
-            src = w1_raw[a][:].rearrange("p j (m t) -> p m j t", t=PACK)[:, :, :, t0:t1]
-            return dst, src
+        def w1_views(a, t0, out):
+            w1_bf[a, t0] = out
+            dst = out[:].rearrange("p (t m j) -> p m j t", t=2, j=PACK)
+            return dst, w1_raw[a][:].rearrange("p j (m t) -> p m j t", t=PACK)[:, :, :, t0 : t0 + 2]
 
-        def w1_quantize(a, t0, t1):
-            width = P * (t1 - t0)
-            codes = sb("w1_codes%d%d" % (a, t0), [P, width], U32)
-            scales = sb("w1_sc%d%d" % (a, t0), [P, width], U8)
+        def w1_quantize(a, t0):
+            codes = sb("w1_codes%d%d" % (a, t0), [P, 2 * P], U32)
+            scales = sb("w1_sc%d%d" % (a, t0), [P, 2 * P], U8)
             nc.vector.quantize_mx(out=codes[:].bitcast(FP8X4), scales=scales[:], in_=w1_bf[a, t0][:])
-            for t in range(t0, t1):
-                cols = slice(P * (t - t0), P * (t - t0 + 1))
-                w1_q[a, t] = (codes[:, cols].bitcast(FP8X4), scales[:, cols])
-
-        direct = {}
-
-        def direct_tile(b, hf, n):
-            acc = bank(b)
-            for a in range(PASSES):
-                first_stage(
-                    acc, w3_codes[:, a, P * n : P * (n + 1)].bitcast(FP8X4),
-                    w3_sc[8 + 4 * a :, P * n : P * (n + 1)], a, hf, 0,
-                )
-            direct[hf, n] = sb("direct%d%d" % (hf, n), [P, HALF], F32)[:]
-            nc.scalar.copy(direct[hf, n], acc[:])
+            for t in range(2):
+                w1_q[a, t0 + t] = (codes[:, P * t : P * (t + 1)].bitcast(FP8X4), scales[:, P * t : P * (t + 1)])
 
         th = {}
 
         def tanh(hf, t, out):
             th[hf, t] = out
-            nc.scalar.activation(out, peer[hf, t][:], TANH, bias=neg_bt[:, t : t + 1], scale=-1.0)
+            nc.scalar.activation(out[:], peer[hf, t][:], TANH, bias=neg_bt[:, t : t + 1], scale=-1.0)
 
-        act = {}
-
-        def act_sum(b, hf, t, first):
-            act[hf, t] = bank(b)
-            for a in (first, 1 - first):
-                first_stage(act[hf, t], w1_q[a, t][0], w1_q[a, t][1], a, hf, first)
-
-        h = [sb("h%d" % hf, [P, PACK, HALF], F32) for hf in range(HALVES)]
+        h = {}
         h_rows = out_1.rearrange("(p t) j -> p t j", t=PACK)
 
-        def subtract(hf, t):
-            nc.vector.scalar_tensor_tensor(h[hf][:, t, :], th[hf, t], gain_sb[:, t : t + 1], act[hf, t][:], MULT, ADD)
+        def unexplained(b, hf, t, first):
+            act = bank(b)
+            for a in (first, 1 - first):
+                first_stage(act, w1_q[a, t][0], w1_q[a, t][1], a, hf, first)
+            nc.vector.scalar_tensor_tensor(h[hf][:, t, :], th[hf, t][:], gain_sb[:, t : t + 1], act[:], MULT, ADD)
             nc.sync.dma_start(out=h_rows[:, t, HALF * hf : HALF * (hf + 1)], in_=h[hf][:, t, :])
 
-        h_bf = [sb("h_bf%d" % hf, [P, PACK * HALF], BF16) for hf in range(HALVES)]
-        h_codes = {}
+        def gpsimd_cast(dst, src):
+            nc.gpsimd.tensor_scalar(dst.rearrange("p (c j) -> p c j", j=PACK), src.rearrange("p j c -> p c j"), 1.0, 0.0, MULT, ADD)
+
+        h_bf = [sb("h_bf%d" % hf, [P, PACK * HALF], BF16) for hf in range(2)]
+
+        def h_cast(hf):
+            nc.scalar.copy(
+                h_bf[hf][:, : PACK * H_SPLIT].rearrange("p (c i t) -> p c t i", i=4, t=PACK),
+                h[hf][:, :, :H_SPLIT].rearrange("p t (c i) -> p c t i", i=4),
+            )
+            gpsimd_cast(h_bf[hf][:, PACK * H_SPLIT :], h[hf][:, :, H_SPLIT:])
+
+        h_codes = [sb("h_codes%d" % hf, [P, HALF], U32) for hf in range(2)]
         h_sc = sb("h_sc", [P, S], U8)
         code_rows = out_2[0].rearrange("p m t -> p (m t)").bitcast(I32)
 
-        def h_views(hf, c0, c1):
-            dst = h_bf[hf][:, PACK * c0 : PACK * c1].rearrange("p (c i t) -> p c t i", i=4, t=PACK)
-            src = h[hf][:, :, c0:c1].rearrange("p t (c i) -> p c t i", i=4)
-            return dst, src
-
-        def h_cast(hf):
-            nc.scalar.copy(*h_views(hf, 0, H_SPLIT))
-            nc.gpsimd.tensor_scalar(
-                h_bf[hf][:, PACK * H_SPLIT :].rearrange("p (c t) -> p c t", t=PACK),
-                h[hf][:, :, H_SPLIT:].rearrange("p t c -> p c t"),
-                1.0, 0.0, MULT, ADD,
-            )
-
         def h_quantize(hf):
-            h_codes[hf] = sb("h_codes%d" % hf, [P, HALF], U32)
-            nc.vector.quantize_mx(
-                out=h_codes[hf][:].bitcast(FP8X4), scales=h_sc[:, HALF * hf : HALF * (hf + 1)], in_=h_bf[hf][:]
-            )
-            nc.sync.dma_start(out=code_rows[:, HALF * hf : HALF * (hf + 1)], in_=h_codes[hf][:].bitcast(I32))
+            cols = slice(HALF * hf, HALF * (hf + 1))
+            nc.vector.quantize_mx(out=h_codes[hf][:].bitcast(FP8X4), scales=h_sc[:, cols], in_=h_bf[hf][:])
+            nc.sync.dma_start(out=code_rows[:, cols], in_=h_codes[hf][:].bitcast(I32))
 
-        def w4_quantize(n0, n1):
-            cols = slice(P * n0, P * n1)
-            nc.vector.quantize_mx(
-                out=w4_codes[:, cols].bitcast(FP8X4), scales=w4_sc[:, cols], in_=w4_bf[:, PACK * P * n0 : PACK * P * n1]
-            )
+        direct = {}
+
+        def direct_tile(b, hf, n):
+            acc = bank(b)
+            cols = slice(P * n, P * (n + 1))
+            for a in range(PASSES):
+                first_stage(acc, w3_codes[:, a, cols].bitcast(FP8X4), w3_sc[8 + 4 * a :, cols], a, hf, 0)
+            direct[hf, n] = sb("direct%d%d" % (hf, n), [P, HALF], F32)
+            nc.scalar.copy(direct[hf, n][:], acc[:])
 
         def ring_tile(b, hf, n):
             acc = bank(b)
+            cols = slice(P * n, P * (n + 1))
             nc.tensor.matmul_mx(
-                out=acc[:],
-                lhsT=w4_codes[:, P * n : P * (n + 1)].bitcast(FP8X4),
-                lhsT_scale=w4_sc[:, P * n : P * (n + 1)],
-                rhs=h_codes[hf][:].bitcast(FP8X4),
-                rhs_scale=h_sc[:, HALF * hf : HALF * (hf + 1)],
-                start=True,
-                stop=True,
+                out=acc[:], lhsT=w4_codes[:, cols].bitcast(FP8X4), lhsT_scale=w4_sc[:, cols],
+                rhs=h_codes[hf][:].bitcast(FP8X4), rhs_scale=h_sc[:, HALF * hf : HALF * (hf + 1)], start=True, stop=True,
             )
-            width = QUARTER if (hf, n) == (HALVES - 1, N_TILES - 1) else HALF
+            width = LAST_PIECE if (hf, n) == (1, N_TILES - 1) else HALF
             for c in range(0, HALF, width):
                 y = sb("y%d%d%d" % (hf, n, c), [P, width], F32)
                 nc.vector.tensor_tensor(y[:], acc[:, c : c + width], direct[hf, n][:, c : c + width], MULT)
-                nc.sync.dma_start(out=out_0[P * n : P * (n + 1), HALF * hf + c : HALF * hf + c + width], in_=y[:])
+                nc.sync.dma_start(out=out_0[cols, HALF * hf + c : HALF * hf + c + width], in_=y[:])
 
         for a in range(PASSES):
-            for hf in range(HALVES):
-                for t in range(PACK):
-                    peer_pass(a, hf, t)
-        nc.vector.tensor_copy(*w1_views(0, 0, 2))
-        nc.scalar.copy(*w1_views(0, 2, 4))
-        w1_quantize(0, 0, 2)
-        w1_quantize(0, 2, 4)
+            for t in range(PACK):
+                peer_pass(a, 0, t, 0)
         for t in range(PACK):
-            tanh(0, t, turns.tile([P, HALF], F32, name="th0%d" % t, offset=4 * H * t, align_bytes=64)[:])
-        nc.vector.tensor_copy(*w1_views(1, 0, 2))
-        nc.vector.tensor_copy(*w1_views(1, 2, 4))
-        w1_quantize(1, 0, 2)
-        w1_quantize(1, 2, 4)
+            for a in (1, 0):
+                peer_pass(a, 1, t, 1)
+        for t0 in (0, 2):
+            nc.vector.tensor_copy(*w1_views(0, t0, sb("w1_bf0%d" % t0, [P, 2 * H], BF16)))
+        for t0 in (0, 2):
+            w1_quantize(0, t0)
+        for t in range(EARLY_TANH):
+            tanh(0, t, sb("th0%d" % t, [P, HALF], F32))
+        nc.vector.tensor_copy(*w1_views(1, 0, sb("w1_bf10", [P, 2 * H], BF16)))
+        nc.scalar.copy(*w1_views(1, 2, placed("w1_bf12", [P, 2 * H], BF16, 8 * SLOT - SLOT // 2)))
+        for t0 in (0, 2):
+            w1_quantize(1, t0)
+        late = [(0, t) for t in range(EARLY_TANH, PACK)] + [(1, t) for t in range(PACK)]
+        for i, (hf, t) in enumerate(late):
+            if i < PACK:
+                tanh(hf, t, placed("th%d%d" % (hf, t), [P, HALF], F32, i * SLOT))
+            else:
+                tanh(hf, t, sb("th%d%d" % (hf, t), [P, HALF], F32, tag="th0%d" % (i - PACK)))
+        h[0] = placed("h0", [P, PACK, HALF], F32, 4 * SLOT)
+        h[1] = sb("h1", [P, PACK, HALF], F32)
+        w4_bf = placed("w4_bf", [P, PACK * N], BF16, 8 * SLOT)
+        gpsimd_cast(w4_bf[:], w4_raw[:])
+
         for t in range(PACK):
-            tanh(1, t, sb("th1%d" % t, [P, HALF], F32)[:])
-        w4_bf = sb("w4_bf", [P, PACK * N], BF16, tag="w1_bf12")
-        nc.gpsimd.tensor_scalar(
-            w4_bf[:].rearrange("p (c j) -> p c j", j=PACK),
-            w4_raw[:].rearrange("p j c -> p c j"),
-            1.0, 0.0, MULT, ADD,
-        )
-        for t in range(PACK):
-            act_sum(t, 0, t, t // 2)
-            subtract(0, t)
+            unexplained(t, 0, t, t // 2)
         h_cast(0)
         for t in range(PACK - 1):
-            act_sum(4 + t, 1, t, 1)
-            subtract(1, t)
+            unexplained(PACK + t, 1, t, 1)
         direct_tile(7, 0, 0)
         direct_tile(0, 0, 1)
-        w4_codes = sb("w4_codes", [P, N], U32, tag="th11")
+        w4_codes = placed("w4_codes", [P, N], U32, (PACK + 1 - EARLY_TANH) * SLOT)
         w4_sc = sb("w4_sc", [P, N], U8)
-        w4_quantize(0, 1)
-        w4_quantize(1, N_TILES)
+        for n0, n1 in ((0, 1), (1, N_TILES)):
+            nc.vector.quantize_mx(
+                out=w4_codes[:, P * n0 : P * n1].bitcast(FP8X4), scales=w4_sc[:, P * n0 : P * n1],
+                in_=w4_bf[:, PACK * P * n0 : PACK * P * n1],
+            )
         h_quantize(0)
-        act_sum(6, 1, 3, 1)
-        subtract(1, 3)
+        unexplained(6, 1, 3, 1)
         h_cast(1)
-        for n in range(2):
-            ring_tile(2 + n, 0, n)
+        ring_tile(2, 0, 0)
+        ring_tile(3, 0, 1)
         direct_tile(1, 0, 2)
         h_quantize(1)
         for r in range(4):

@@ -27,7 +27,6 @@ SC = H + S
 H_SPLIT = 288
 LAST_PIECE = 256
 SLOT = 4 * HALF
-EARLY_TANH = 3
 
 
 def tile_list_fraud_ring_cards_kernel(
@@ -71,7 +70,6 @@ def tile_list_fraud_ring_cards_kernel(
         bt_sb = sb("bt_sb", [P, PACK], F32)
         gain_sb = sb("gain_sb", [P, PACK], F32)
         nc.scalar.dma_start(out=bt_sb[:], in_=bt.rearrange("(p t) -> p t", t=PACK))
-        nc.scalar.dma_start(out=gain_sb[:], in_=gain.rearrange("(p t) -> p t", t=PACK))
         neg_bt = sb("neg_bt", [P, PACK], F32)
         nc.scalar.mul(neg_bt[:], bt_sb[:], -1.0)
         w2_raw = sb("w2_raw", [P, PASSES, 2 * H], U8)
@@ -94,12 +92,12 @@ def tile_list_fraud_ring_cards_kernel(
                 load_bytes(planes[a][r:P:32, :], sc_rows[first_row + r : first_row + 16 : 4, :])
 
         w1_rows = w1.rearrange("(a p j) c -> a p j c", a=PASSES, j=PACK)
-        w1_raw = [sb("w1_raw0", [P, PACK, H], F32), placed("w1_raw1", [P, PACK, H], F32, 0)]
+        w1_raw = [placed("w1_raw0", [P, PACK, H], F32, 0), sb("w1_raw1", [P, PACK, H], F32)]
         move_to_planes(0)
-        load(w1_raw[0][:, 0:2, :], w1_rows[0][:, 0:2, :])
+        load(w1_raw[0][:], w1_rows[0])
         move_to_planes(1)
-        load(w1_raw[0][:, 2:4, :], w1_rows[0][:, 2:4, :])
         load(w1_raw[1][:], w1_rows[1])
+        load(gain_sb[:], gain.rearrange("(p t) -> p t", t=PACK))
         w4_raw = sb("w4_raw", [P, PACK, N], F32)
         load(w4_raw[:], w4.rearrange("(p j) n -> p j n", j=PACK))
         for q in range(4):
@@ -212,30 +210,24 @@ def tile_list_fraud_ring_cards_kernel(
                 nc.sync.dma_start(out=out_0[cols, HALF * hf + c : HALF * hf + c + width], in_=y[:])
 
         for a in range(PASSES):
-            for t in range(PACK):
-                peer_pass(a, 0, t, 0)
-        for t in range(PACK):
-            for a in (1, 0):
-                peer_pass(a, 1, t, 1)
-        for t0 in (0, 2):
-            nc.vector.tensor_copy(*w1_views(0, t0, sb("w1_bf0%d" % t0, [P, 2 * H], BF16)))
+            for hf in range(2):
+                for t in range(PACK):
+                    peer_pass(a, hf, t, 0)
+        nc.vector.tensor_copy(*w1_views(0, 0, sb("w1_bf00", [P, 2 * H], BF16)))
+        nc.scalar.copy(*w1_views(0, 2, sb("w1_bf02", [P, 2 * H], BF16)))
         for t0 in (0, 2):
             w1_quantize(0, t0)
-        for t in range(EARLY_TANH):
-            tanh(0, t, sb("th0%d" % t, [P, HALF], F32))
-        nc.vector.tensor_copy(*w1_views(1, 0, sb("w1_bf10", [P, 2 * H], BF16)))
-        nc.scalar.copy(*w1_views(1, 2, placed("w1_bf12", [P, 2 * H], BF16, 8 * SLOT - SLOT // 2)))
+        for t in range(PACK):
+            tanh(0, t, placed("th0%d" % t, [P, HALF], F32, t * SLOT))
+        for t0 in (0, 2):
+            nc.vector.tensor_copy(*w1_views(1, t0, sb("w1_bf1%d" % t0, [P, 2 * H], BF16)))
         for t0 in (0, 2):
             w1_quantize(1, t0)
-        late = [(0, t) for t in range(EARLY_TANH, PACK)] + [(1, t) for t in range(PACK)]
-        for i, (hf, t) in enumerate(late):
-            if i < PACK:
-                tanh(hf, t, placed("th%d%d" % (hf, t), [P, HALF], F32, i * SLOT))
-            else:
-                tanh(hf, t, sb("th%d%d" % (hf, t), [P, HALF], F32, tag="th0%d" % (i - PACK)))
-        h[0] = placed("h0", [P, PACK, HALF], F32, 4 * SLOT)
-        h[1] = sb("h1", [P, PACK, HALF], F32)
-        w4_bf = placed("w4_bf", [P, PACK * N], BF16, 8 * SLOT)
+        for t in range(PACK):
+            tanh(1, t, sb("th1%d" % t, [P, HALF], F32))
+        for hf in range(2):
+            h[hf] = sb("h%d" % hf, [P, PACK, HALF], F32)
+        w4_bf = sb("w4_bf", [P, PACK * N], BF16, tag="w1_bf12")
         gpsimd_cast(w4_bf[:], w4_raw[:])
 
         for t in range(PACK):
@@ -245,7 +237,7 @@ def tile_list_fraud_ring_cards_kernel(
             unexplained(PACK + t, 1, t, 1)
         direct_tile(7, 0, 0)
         direct_tile(0, 0, 1)
-        w4_codes = placed("w4_codes", [P, N], U32, (PACK + 1 - EARLY_TANH) * SLOT)
+        w4_codes = sb("w4_codes", [P, N], U32, tag="th11")
         w4_sc = sb("w4_sc", [P, N], U8)
         for n0, n1 in ((0, 1), (1, N_TILES)):
             nc.vector.quantize_mx(

@@ -27,6 +27,7 @@ SC = H + S
 H_SPLIT = 288
 LAST_PIECE = 256
 SLOT = 4 * HALF
+ALIGN = 256
 
 
 def tile_list_fraud_ring_cards_kernel(
@@ -40,10 +41,10 @@ def tile_list_fraud_ring_cards_kernel(
         psum = ctx.enter_context(tc.psum_pool(name="psum", bufs=1))
 
         def sb(name, shape, dtype, tag=None):
-            return keep.tile(shape, dtype, name=name, tag=tag or name, align_bytes=64)
+            return keep.tile(shape, dtype, name=name, tag=tag or name, align_bytes=ALIGN)
 
         def placed(name, shape, dtype, offset):
-            return turns.tile(shape, dtype, name=name, offset=offset, align_bytes=64)
+            return turns.tile(shape, dtype, name=name, offset=offset, align_bytes=ALIGN)
 
         def bank(b):
             return psum.tile([P, HALF], F32, name="bank%d" % b)
@@ -69,14 +70,14 @@ def tile_list_fraud_ring_cards_kernel(
         load_bytes(w2_sc[ROWS_AT:, :], w2_scales.rearrange("a q c -> (a q) c"))
         bt_sb = sb("bt_sb", [P, PACK], F32)
         gain_sb = sb("gain_sb", [P, PACK], F32)
-        nc.scalar.dma_start(out=bt_sb[:], in_=bt.rearrange("(p t) -> p t", t=PACK))
-        neg_bt = sb("neg_bt", [P, PACK], F32)
-        nc.scalar.mul(neg_bt[:], bt_sb[:], -1.0)
         w2_raw = sb("w2_raw", [P, PASSES, 2 * H], U8)
         load_bytes(w2_raw[:], w2_words.rearrange("a p c -> p a c"))
         tab = [sb("tab%d" % a, [P, T], I32) for a in range(PASSES)]
         for a in range(PASSES):
             load(tab[a][:], tab_words[a].rearrange("p t i -> p (t i)").bitcast(I32))
+        load(bt_sb[:], bt.rearrange("(p t) -> p t", t=PACK))
+        neg_bt = sb("neg_bt", [P, PACK], F32)
+        nc.scalar.mul(neg_bt[:], bt_sb[:], -1.0)
 
         picked_sc = sb("picked_sc", [P, S], U8)
         nc.vector.tensor_copy(picked_sc[:], tab_sc[:].indirect(offsets[:]))

@@ -1,6 +1,7 @@
 from contextlib import ExitStack
 
 import concourse.mybir as mybir
+from concourse.masks import make_identity
 
 K, T, S, H, N = 1024, 2048, 1024, 512, 384
 FLOPS = 2 * S * (2 * K * H + K * N + H * N)
@@ -64,20 +65,28 @@ def tile_list_fraud_ring_cards_kernel(
         w3_sc = sb("w3_sc", [P, N], U8)
         for zeroed in planes + [w3_sc]:
             nc.gpsimd.memset(zeroed[:].bitcast(I32), 0)
+        vectors = sb("vectors", [P, H], F32)
+        nc.vector.memset(vectors[:], 0.0)
+        identity = sb("identity", [P, P], F32)
+        make_identity(nc, identity[:])
 
         load_bytes(tab_sc[ROWS_AT:, :], tab_scales.rearrange("a q c -> (a q) c"))
         nc.sync.dma_start(offsets[:], offs)
         load_bytes(w2_sc[ROWS_AT:, :], w2_scales.rearrange("a q c -> (a q) c"))
-        bt_sb = sb("bt_sb", [P, PACK], F32)
         gain_sb = sb("gain_sb", [P, PACK], F32)
         w2_raw = sb("w2_raw", [P, PASSES, 2 * H], U8)
         load_bytes(w2_raw[:], w2_words.rearrange("a p c -> p a c"))
         tab = [sb("tab%d" % a, [P, T], I32) for a in range(PASSES)]
-        for a in range(PASSES):
-            load(tab[a][:], tab_words[a].rearrange("p t i -> p (t i)").bitcast(I32))
-        load(bt_sb[:], bt.rearrange("(p t) -> p t", t=PACK))
+        load(tab[0][:], tab_words[0].rearrange("p t i -> p (t i)").bitcast(I32))
+        for row, vector in enumerate((bt, gain)):
+            load(vectors[row : row + 1, :], vector.unsqueeze(0))
+        load(tab[1][:], tab_words[1].rearrange("p t i -> p (t i)").bitcast(I32))
+        turned = bank(7)
+        for t in range(PACK):
+            nc.tensor.transpose(turned[:, P * t : P * (t + 1)], vectors[:, t:H:PACK], identity[:])
         neg_bt = sb("neg_bt", [P, PACK], F32)
-        nc.scalar.mul(neg_bt[:], bt_sb[:], -1.0)
+        nc.scalar.mul(neg_bt[:], turned[:, 0:HALF:P], -1.0)
+        nc.scalar.copy(gain_sb[:], turned[:, 1:HALF:P])
 
         picked_sc = sb("picked_sc", [P, S], U8)
         nc.vector.tensor_copy(picked_sc[:], tab_sc[:].indirect(offsets[:]))
@@ -98,7 +107,6 @@ def tile_list_fraud_ring_cards_kernel(
         load(w1_raw[0][:], w1_rows[0])
         move_to_planes(1)
         load(w1_raw[1][:], w1_rows[1])
-        load(gain_sb[:], gain.rearrange("(p t) -> p t", t=PACK))
         w4_raw = sb("w4_raw", [P, PACK, N], F32)
         load(w4_raw[:], w4.rearrange("(p j) n -> p j n", j=PACK))
         for q in range(4):

@@ -25,10 +25,14 @@ HALF = S // 2
 N_TILES = N // P
 ROWS_AT = 96
 SC = H + S
-H_SPLIT = 288
+H_SPLIT = (320, 288)
 LAST_PIECE = 256
 SLOT = 4 * HALF
+RAW1_AT = PACK * SLOT
+M_SPLIT = 64
+EARLY_PEERS = [(0, t) for t in range(PACK)] + [(1, t) for t in range(2)]
 ALIGN = 256
+LATE_AT = RAW1_AT + ALIGN - SLOT
 
 
 def tile_list_fraud_ring_cards_kernel(
@@ -59,14 +63,14 @@ def tile_list_fraud_ring_cards_kernel(
         offsets = keep.tile([P, S // 16], U16, name="offsets")
         tab_sc = sb("tab_sc", [P, T], U8)
         w2_sc = sb("w2_sc", [P, H], U8)
-        for rows in (tab_sc, w2_sc):
-            nc.vector.memset(rows[0:ROWS_AT, :].bitcast(I32), 0)
+        nc.vector.memset(tab_sc[0:ROWS_AT, :].bitcast(I32), 0)
+        nc.gpsimd.memset(w2_sc[0:ROWS_AT, :].bitcast(I32), 0)
         planes = [sb("planes%d" % a, [P, SC], U8) for a in range(PASSES)]
         w3_sc = sb("w3_sc", [P, N], U8)
         for zeroed in planes + [w3_sc]:
             nc.gpsimd.memset(zeroed[:].bitcast(I32), 0)
         vectors = sb("vectors", [P, H], F32)
-        nc.vector.memset(vectors[:], 0.0)
+        nc.gpsimd.memset(vectors[:], 0.0)
         identity = sb("identity", [P, P], F32)
         make_identity(nc, identity[:])
 
@@ -102,7 +106,7 @@ def tile_list_fraud_ring_cards_kernel(
                 load_bytes(planes[a][r:P:32, :], sc_rows[first_row + r : first_row + 16 : 4, :])
 
         w1_rows = w1.rearrange("(a p j) c -> a p j c", a=PASSES, j=PACK)
-        w1_raw = [placed("w1_raw0", [P, PACK, H], F32, 0), sb("w1_raw1", [P, PACK, H], F32)]
+        w1_raw = [placed("w1_raw0", [P, PACK, H], F32, 0), placed("w1_raw1", [P, PACK, H], F32, RAW1_AT)]
         move_to_planes(0)
         load(w1_raw[0][:], w1_rows[0])
         move_to_planes(1)
@@ -135,6 +139,13 @@ def tile_list_fraud_ring_cards_kernel(
                 rhs_scale=planes[a][:, H + HALF * hf : H + HALF * (hf + 1)], start=(a == first), stop=(a != first),
             )
 
+        warm = bank(6)
+        for w in range(4):
+            nc.tensor.matmul_mx(
+                out=warm[:], lhsT=tab[0][:, 0:P].bitcast(FP8X4), lhsT_scale=picked_sc[:, 0:P],
+                rhs=tab[0][:, 0:HALF].bitcast(FP8X4), rhs_scale=picked_sc[:, 0:HALF], start=True, stop=True,
+            )
+
         peer = {}
 
         def peer_pass(a, hf, t, first):
@@ -146,17 +157,21 @@ def tile_list_fraud_ring_cards_kernel(
         w1_bf = {}
         w1_q = {}
 
-        def w1_views(a, t0, out):
-            w1_bf[a, t0] = out
-            dst = out[:].rearrange("p (t m j) -> p m j t", t=2, j=PACK)
-            return dst, w1_raw[a][:].rearrange("p j (m t) -> p m j t", t=PACK)[:, :, :, t0 : t0 + 2]
+        def w1_views(a, t0, m0=0, m1=P):
+            dst = w1_bf[a, t0][:].rearrange("p (t m j) -> p m j t", t=2, j=PACK)
+            src = w1_raw[a][:].rearrange("p j (m t) -> p m j t", t=PACK)
+            return dst[:, m0:m1], src[:, m0:m1, :, t0 : t0 + 2]
 
-        def w1_quantize(a, t0):
-            codes = sb("w1_codes%d%d" % (a, t0), [P, 2 * P], U32)
-            scales = sb("w1_sc%d%d" % (a, t0), [P, 2 * P], U8)
-            nc.vector.quantize_mx(out=codes[:].bitcast(FP8X4), scales=scales[:], in_=w1_bf[a, t0][:])
-            for t in range(2):
-                w1_q[a, t0 + t] = (codes[:, P * t : P * (t + 1)].bitcast(FP8X4), scales[:, P * t : P * (t + 1)])
+        def w1_quantize(a, t0, t1):
+            width = P * (t1 - t0)
+            codes = sb("w1_codes%d%d" % (a, t0), [P, width], U32)
+            scales = sb("w1_sc%d%d" % (a, t0), [P, width], U8)
+            pair = t0 - t0 % 2
+            source = w1_bf[a, pair][:, H * (t0 - pair) : H * (t1 - pair)]
+            nc.vector.quantize_mx(out=codes[:].bitcast(FP8X4), scales=scales[:], in_=source)
+            for t in range(t0, t1):
+                cols = slice(P * (t - t0), P * (t - t0 + 1))
+                w1_q[a, t] = (codes[:, cols].bitcast(FP8X4), scales[:, cols])
 
         th = {}
 
@@ -177,14 +192,16 @@ def tile_list_fraud_ring_cards_kernel(
         def gpsimd_cast(dst, src):
             nc.gpsimd.tensor_scalar(dst.rearrange("p (c j) -> p c j", j=PACK), src.rearrange("p j c -> p c j"), 1.0, 0.0, MULT, ADD)
 
-        h_bf = [sb("h_bf%d" % hf, [P, PACK * HALF], BF16) for hf in range(2)]
+        h_bf = {}
 
         def h_cast(hf):
+            split = H_SPLIT[hf]
+            h_bf[hf] = sb("h_bf%d" % hf, [P, PACK * HALF], BF16, tag="h_bf")
             nc.scalar.copy(
-                h_bf[hf][:, : PACK * H_SPLIT].rearrange("p (c i t) -> p c t i", i=4, t=PACK),
-                h[hf][:, :, :H_SPLIT].rearrange("p t (c i) -> p c t i", i=4),
+                h_bf[hf][:, : PACK * split].rearrange("p (c i t) -> p c t i", i=4, t=PACK),
+                h[hf][:, :, :split].rearrange("p t (c i) -> p c t i", i=4),
             )
-            gpsimd_cast(h_bf[hf][:, PACK * H_SPLIT :], h[hf][:, :, H_SPLIT:])
+            gpsimd_cast(h_bf[hf][:, PACK * split :], h[hf][:, :, split:])
 
         h_codes = [sb("h_codes%d" % hf, [P, HALF], U32) for hf in range(2)]
         h_sc = sb("h_sc", [P, S], U8)
@@ -212,28 +229,36 @@ def tile_list_fraud_ring_cards_kernel(
                 out=acc[:], lhsT=w4_codes[:, cols].bitcast(FP8X4), lhsT_scale=w4_sc[:, cols],
                 rhs=h_codes[hf][:].bitcast(FP8X4), rhs_scale=h_sc[:, HALF * hf : HALF * (hf + 1)], start=True, stop=True,
             )
-            width = LAST_PIECE if (hf, n) == (1, N_TILES - 1) else HALF
-            for c in range(0, HALF, width):
-                y = sb("y%d%d%d" % (hf, n, c), [P, width], F32)
-                nc.vector.tensor_tensor(y[:], acc[:, c : c + width], direct[hf, n][:, c : c + width], MULT)
-                nc.sync.dma_start(out=out_0[cols, HALF * hf + c : HALF * hf + c + width], in_=y[:])
+            cuts = (0, HALF - LAST_PIECE, HALF) if (hf, n) == (1, N_TILES - 1) else (0, HALF)
+            for c0, c1 in zip(cuts, cuts[1:]):
+                y = sb("y%d%d%d" % (hf, n, c0), [P, c1 - c0], F32)
+                nc.vector.tensor_tensor(y[:], acc[:, c0:c1], direct[hf, n][:, c0:c1], MULT)
+                nc.sync.dma_start(out=out_0[cols, HALF * hf + c0 : HALF * hf + c1], in_=y[:])
 
         for a in range(PASSES):
-            for hf in range(2):
-                for t in range(PACK):
-                    peer_pass(a, hf, t, 0)
-        nc.vector.tensor_copy(*w1_views(0, 0, sb("w1_bf00", [P, 2 * H], BF16)))
-        nc.scalar.copy(*w1_views(0, 2, sb("w1_bf02", [P, 2 * H], BF16)))
+            for hf, t in EARLY_PEERS:
+                peer_pass(a, hf, t, 0)
+        for t in range(2, PACK):
+            for a in (1, 0):
+                peer_pass(a, 1, t, 1)
+        for a in range(PASSES):
+            for t0 in (0, 2):
+                w1_bf[a, t0] = sb("w1_bf%d%d" % (a, t0), [P, 2 * H], BF16)
+        nc.vector.tensor_copy(*w1_views(0, 0))
+        nc.scalar.copy(*w1_views(0, 2))
         for t0 in (0, 2):
-            w1_quantize(0, t0)
-        for t in range(PACK):
+            w1_quantize(0, t0, t0 + 2)
+        for t in range(2):
             tanh(0, t, placed("th0%d" % t, [P, HALF], F32, t * SLOT))
+        nc.scalar.copy(*w1_views(1, 0, M_SPLIT, P))
         for t0 in (0, 2):
-            nc.vector.tensor_copy(*w1_views(1, t0, sb("w1_bf1%d" % t0, [P, 2 * H], BF16)))
-        for t0 in (0, 2):
-            w1_quantize(1, t0)
-        for t in range(PACK):
-            tanh(1, t, sb("th1%d" % t, [P, HALF], F32))
+            nc.vector.tensor_copy(*w1_views(1, t0, 0, M_SPLIT))
+        w1_quantize(1, 0, 2)
+        nc.vector.tensor_copy(*w1_views(1, 2, M_SPLIT, P))
+        w1_quantize(1, 2, 4)
+        for i, (hf, t) in enumerate(((0, 2), (0, 3), (1, 0), (1, 1), (1, 2))):
+            tanh(hf, t, placed("th%d%d" % (hf, t), [P, HALF], F32, LATE_AT + i * SLOT))
+        tanh(1, 3, sb("th13", [P, HALF], F32, tag="w1_bf10"))
         for hf in range(2):
             h[hf] = sb("h%d" % hf, [P, PACK, HALF], F32)
         w4_bf = sb("w4_bf", [P, PACK * N], BF16, tag="w1_bf12")
@@ -246,13 +271,9 @@ def tile_list_fraud_ring_cards_kernel(
             unexplained(PACK + t, 1, t, 1)
         direct_tile(7, 0, 0)
         direct_tile(0, 0, 1)
-        w4_codes = sb("w4_codes", [P, N], U32, tag="th11")
+        w4_codes = placed("w4_codes", [P, N], U32, LATE_AT + 3 * SLOT)
         w4_sc = sb("w4_sc", [P, N], U8)
-        for n0, n1 in ((0, 1), (1, N_TILES)):
-            nc.vector.quantize_mx(
-                out=w4_codes[:, P * n0 : P * n1].bitcast(FP8X4), scales=w4_sc[:, P * n0 : P * n1],
-                in_=w4_bf[:, PACK * P * n0 : PACK * P * n1],
-            )
+        nc.vector.quantize_mx(out=w4_codes[:].bitcast(FP8X4), scales=w4_sc[:], in_=w4_bf[:])
         h_quantize(0)
         unexplained(6, 1, 3, 1)
         h_cast(1)

@@ -139,13 +139,6 @@ def tile_list_fraud_ring_cards_kernel(
                 rhs_scale=planes[a][:, H + HALF * hf : H + HALF * (hf + 1)], start=(a == first), stop=(a != first),
             )
 
-        warm = bank(6)
-        for w in range(4):
-            nc.tensor.matmul_mx(
-                out=warm[:], lhsT=tab[0][:, 0:P].bitcast(FP8X4), lhsT_scale=picked_sc[:, 0:P],
-                rhs=tab[0][:, 0:HALF].bitcast(FP8X4), rhs_scale=picked_sc[:, 0:HALF], start=True, stop=True,
-            )
-
         peer = {}
 
         def peer_pass(a, hf, t, first):

@@ -70,7 +70,7 @@ def tile_list_fraud_ring_cards_kernel(
         for zeroed in planes + [w3_sc]:
             nc.gpsimd.memset(zeroed[:].bitcast(I32), 0)
         vectors = sb("vectors", [P, H], F32)
-        nc.gpsimd.memset(vectors[:], 0.0)
+        nc.vector.memset(vectors[:], 0.0)
         identity = sb("identity", [P, P], F32)
         make_identity(nc, identity[:])
 

@@ -25,7 +25,7 @@ HALF = S // 2
 N_TILES = N // P
 ROWS_AT = 96
 SC = H + S
-H_SPLIT = (320, 288)
+H_SPLIT = (288, 288)
 LAST_PIECE = 256
 SLOT = 4 * HALF
 RAW1_AT = PACK * SLOT
@@ -125,7 +125,7 @@ def tile_list_fraud_ring_cards_kernel(
             nc.vector.tensor_copy(v[a, hf], tab[a][:].bitcast(U32).indirect(offsets[:, 32 * hf : 32 * (hf + 1)]))
 
         w2_codes = sb("w2_codes", [P, PASSES, 2 * H], U8)
-        nc.vector.tensor_copy(
+        nc.scalar.copy(
             w2_codes[:].bitcast(U16).rearrange("p a (t m) -> p a t m", t=PACK),
             w2_raw[:].bitcast(U16).rearrange("p a (m t) -> p a t m", t=PACK),
         )
@@ -246,7 +246,8 @@ def tile_list_fraud_ring_cards_kernel(
         nc.scalar.copy(*w1_views(1, 0, M_SPLIT, P))
         for t0 in (0, 2):
             nc.vector.tensor_copy(*w1_views(1, t0, 0, M_SPLIT))
-        w1_quantize(1, 0, 2)
+        w1_quantize(1, 0, 1)
+        w1_quantize(1, 1, 2)
         nc.vector.tensor_copy(*w1_views(1, 2, M_SPLIT, P))
         w1_quantize(1, 2, 4)
         for i, (hf, t) in enumerate(((0, 2), (0, 3), (1, 0), (1, 1), (1, 2))):
@@ -258,7 +259,7 @@ def tile_list_fraud_ring_cards_kernel(
         gpsimd_cast(w4_bf[:], w4_raw[:])
 
         for t in range(PACK):
-            unexplained(t, 0, t, t // 2)
+            unexplained(t, 0, t, 0)
         h_cast(0)
         for t in range(PACK - 1):
             unexplained(PACK + t, 1, t, 1)

@@ -98,7 +98,7 @@ def tile_list_fraud_ring_cards_kernel(
         nc.vector.tensor_copy(
             sc_rows[:, 0:H].rearrange("p (t m) -> p t m", t=PACK), w2_sc[:].rearrange("p (m t) -> p t m", t=PACK)
         )
-        nc.vector.tensor_copy(sc_rows[ROWS_AT:, H:SC].bitcast(I32), picked_sc[ROWS_AT:, :].bitcast(I32))
+        nc.vector.tensor_copy(sc_rows[:, H:SC].bitcast(I32), picked_sc[:].bitcast(I32))
 
         def move_to_planes(a):
             first_row = ROWS_AT + 16 * a

@@ -30,6 +30,7 @@ LAST_PIECE = 256
 SLOT = 4 * HALF
 RAW1_AT = PACK * SLOT
 M_SPLIT = 64
+M_EARLY = 96
 EARLY_PEERS = [(0, t) for t in range(PACK)] + [(1, t) for t in range(2)]
 ALIGN = 256
 LATE_AT = RAW1_AT + ALIGN - SLOT
@@ -108,8 +109,9 @@ def tile_list_fraud_ring_cards_kernel(
         w1_rows = w1.rearrange("(a p j) c -> a p j c", a=PASSES, j=PACK)
         w1_raw = [placed("w1_raw0", [P, PACK, H], F32, 0), placed("w1_raw1", [P, PACK, H], F32, RAW1_AT)]
         move_to_planes(0)
-        load(w1_raw[0][:], w1_rows[0])
+        load(w1_raw[0][:, : PACK - 1], w1_rows[0][:, : PACK - 1])
         move_to_planes(1)
+        load(w1_raw[0][:, PACK - 1 :], w1_rows[0][:, PACK - 1 :])
         load(w1_raw[1][:], w1_rows[1])
         w4_raw = sb("w4_raw", [P, PACK, N], F32)
         load(w4_raw[:], w4.rearrange("(p j) n -> p j n", j=PACK))
@@ -234,13 +236,14 @@ def tile_list_fraud_ring_cards_kernel(
         for t in range(2, PACK):
             for a in (1, 0):
                 peer_pass(a, 1, t, 1)
-        for a in range(PASSES):
-            for t0 in (0, 2):
-                w1_bf[a, t0] = sb("w1_bf%d%d" % (a, t0), [P, 2 * H], BF16)
-        nc.vector.tensor_copy(*w1_views(0, 0))
-        nc.scalar.copy(*w1_views(0, 2))
+        w1_bf[0, 0] = sb("w1_bf0", [P, PACK * H], BF16)
         for t0 in (0, 2):
-            w1_quantize(0, t0, t0 + 2)
+            w1_bf[1, t0] = sb("w1_bf1%d" % t0, [P, 2 * H], BF16)
+        dst0 = w1_bf[0, 0][:].rearrange("p (t m j) -> p m j t", t=PACK, j=PACK)
+        src0 = w1_raw[0][:].rearrange("p j (m t) -> p m j t", t=PACK)
+        nc.scalar.copy(dst0[:, M_EARLY:], src0[:, M_EARLY:])
+        nc.vector.tensor_copy(dst0[:, :M_EARLY], src0[:, :M_EARLY])
+        w1_quantize(0, 0, PACK)
         for t in range(2):
             tanh(0, t, placed("th0%d" % t, [P, HALF], F32, t * SLOT))
         nc.scalar.copy(*w1_views(1, 0, M_SPLIT, P))
@@ -259,7 +262,7 @@ def tile_list_fraud_ring_cards_kernel(
         gpsimd_cast(w4_bf[:], w4_raw[:])
 
         for t in range(PACK):
-            unexplained(t, 0, t, 0)
+            unexplained(t, 0, t, min(t, 1))
         h_cast(0)
         for t in range(PACK - 1):
             unexplained(PACK + t, 1, t, 1)
@@ -271,7 +274,7 @@ def tile_list_fraud_ring_cards_kernel(
         h_quantize(0)
         unexplained(6, 1, 3, 1)
         h_cast(1)
-        ring_tile(2, 0, 0)
+        ring_tile(7, 0, 0)
         ring_tile(3, 0, 1)
         direct_tile(1, 0, 2)
         h_quantize(1)
@@ -279,8 +282,8 @@ def tile_list_fraud_ring_cards_kernel(
             nc.sync.dma_start(out=out_3[0][r:16:4, :].bitcast(I32), in_=h_sc[r:P:32, :].bitcast(I32))
         ring_tile(4, 0, 2)
         direct_tile(5, 1, 0)
-        direct_tile(7, 1, 1)
+        direct_tile(2, 1, 1)
         ring_tile(0, 1, 0)
         direct_tile(6, 1, 2)
         ring_tile(1, 1, 1)
-        ring_tile(2, 1, 2)
+        ring_tile(7, 1, 2)

@@ -25,7 +25,7 @@ HALF = S // 2
 N_TILES = N // P
 ROWS_AT = 96
 SC = H + S
-H_SPLIT = (288, 288)
+H_SPLIT = (288, 320)
 LAST_PIECE = 256
 SLOT = 4 * HALF
 RAW1_AT = PACK * SLOT
@@ -181,7 +181,11 @@ def tile_list_fraud_ring_cards_kernel(
             act = bank(b)
             for a in (first, 1 - first):
                 first_stage(act, w1_q[a, t][0], w1_q[a, t][1], a, hf, first)
-            nc.vector.scalar_tensor_tensor(h[hf][:, t, :], th[hf, t][:], gain_sb[:, t : t + 1], act[:], MULT, ADD)
+            cuts = (0, H_SPLIT[hf], HALF) if (hf, t) == (1, PACK - 1) else (0, HALF)
+            for c0, c1 in zip(cuts, cuts[1:]):
+                nc.vector.scalar_tensor_tensor(
+                    h[hf][:, t, c0:c1], th[hf, t][:, c0:c1], gain_sb[:, t : t + 1], act[:, c0:c1], MULT, ADD
+                )
             nc.sync.dma_start(out=h_rows[:, t, HALF * hf : HALF * (hf + 1)], in_=h[hf][:, t, :])
 
         def gpsimd_cast(dst, src):
@@ -246,12 +250,11 @@ def tile_list_fraud_ring_cards_kernel(
         w1_quantize(0, 0, PACK)
         for t in range(2):
             tanh(0, t, placed("th0%d" % t, [P, HALF], F32, t * SLOT))
-        nc.scalar.copy(*w1_views(1, 0, M_SPLIT, P))
-        for t0 in (0, 2):
-            nc.vector.tensor_copy(*w1_views(1, t0, 0, M_SPLIT))
+        nc.scalar.copy(*w1_views(1, 2, M_SPLIT, P))
+        nc.vector.tensor_copy(*w1_views(1, 0))
+        nc.vector.tensor_copy(*w1_views(1, 2, 0, M_SPLIT))
         w1_quantize(1, 0, 1)
         w1_quantize(1, 1, 2)
-        nc.vector.tensor_copy(*w1_views(1, 2, M_SPLIT, P))
         w1_quantize(1, 2, 4)
         for i, (hf, t) in enumerate(((0, 2), (0, 3), (1, 0), (1, 1), (1, 2))):
             tanh(hf, t, placed("th%d%d" % (hf, t), [P, HALF], F32, LATE_AT + i * SLOT))
@@ -275,7 +278,7 @@ def tile_list_fraud_ring_cards_kernel(
         unexplained(6, 1, 3, 1)
         h_cast(1)
         ring_tile(7, 0, 0)
-        ring_tile(3, 0, 1)
+        ring_tile(0, 0, 1)
         direct_tile(1, 0, 2)
         h_quantize(1)
         for r in range(4):
@@ -283,7 +286,7 @@ def tile_list_fraud_ring_cards_kernel(
         ring_tile(4, 0, 2)
         direct_tile(5, 1, 0)
         direct_tile(2, 1, 1)
-        ring_tile(0, 1, 0)
+        ring_tile(3, 1, 0)
         direct_tile(6, 1, 2)
         ring_tile(1, 1, 1)
         ring_tile(7, 1, 2)

from contextlib import ExitStack

import concourse.mybir as mybir
from concourse.masks import make_identity

K, T, S, H, N = 1024, 2048, 1024, 512, 384
FLOPS = 2 * S * (2 * K * H + K * N + H * N)

F32 = mybir.dt.float32
BF16 = mybir.dt.bfloat16
I32 = mybir.dt.int32
U32 = mybir.dt.uint32
U16 = mybir.dt.uint16
U8 = mybir.dt.uint8
FP8X4 = mybir.dt.float8_e4m3fn_x4
FP4X4 = mybir.dt.float4_e2m1fn_x4
MULT = mybir.AluOpType.mult
ADD = mybir.AluOpType.add
TANH = mybir.ActivationFunctionType.Tanh

P = 128
PACK = 4
PASSES = K // (P * PACK)
HALF = S // 2
N_TILES = N // P
ROWS_AT = 96
SC = H + S
H_SPLIT = (288, 320)
LAST_PIECE = 256
SLOT = 4 * HALF
RAW1_AT = PACK * SLOT
M_SPLIT = 64
M_EARLY = 96
EARLY_PEERS = [(0, t) for t in range(PACK)] + [(1, t) for t in range(2)]
ALIGN = 256
LATE_AT = RAW1_AT + ALIGN - SLOT


def tile_list_fraud_ring_cards_kernel(
    tc, tab_words, tab_scales, offs, w1, w2_words, w2_scales, bt, gain, w3_words, w3_scales, w4,
    out_0, out_1, out_2, out_3,
):
    nc = tc.nc
    with ExitStack() as ctx:
        keep = ctx.enter_context(tc.tile_pool(name="keep", bufs=1))
        turns = ctx.enter_context(tc.tile_pool(name="turns", bufs=1))
        psum = ctx.enter_context(tc.psum_pool(name="psum", bufs=1))

        def sb(name, shape, dtype, tag=None):
            return keep.tile(shape, dtype, name=name, tag=tag or name, align_bytes=ALIGN)

        def placed(name, shape, dtype, offset):
            return turns.tile(shape, dtype, name=name, offset=offset, align_bytes=ALIGN)

        def bank(b):
            return psum.tile([P, HALF], F32, name="bank%d" % b)

        def load(tile, source):
            nc.sync.dma_start(out=tile, in_=source)

        def load_bytes(tile, source):
            load(tile.bitcast(I32), source.bitcast(I32))

        offsets = keep.tile([P, S // 16], U16, name="offsets")
        tab_sc = sb("tab_sc", [P, T], U8)
        w2_sc = sb("w2_sc", [P, H], U8)
        nc.vector.memset(tab_sc[0:ROWS_AT, :].bitcast(I32), 0)
        nc.gpsimd.memset(w2_sc[0:ROWS_AT, :].bitcast(I32), 0)
        planes = [sb("planes%d" % a, [P, SC], U8) for a in range(PASSES)]
        w3_sc = sb("w3_sc", [P, N], U8)
        for zeroed in planes + [w3_sc]:
            nc.gpsimd.memset(zeroed[:].bitcast(I32), 0)
        vectors = sb("vectors", [P, H], F32)
        nc.vector.memset(vectors[:], 0.0)
        identity = sb("identity", [P, P], F32)
        make_identity(nc, identity[:])

        load_bytes(tab_sc[ROWS_AT:, :], tab_scales.rearrange("a q c -> (a q) c"))
        nc.sync.dma_start(offsets[:], offs)
        load_bytes(w2_sc[ROWS_AT:, :], w2_scales.rearrange("a q c -> (a q) c"))
        gain_sb = sb("gain_sb", [P, PACK], F32)
        w2_raw = sb("w2_raw", [P, PASSES, 2 * H], U8)
        load_bytes(w2_raw[:], w2_words.rearrange("a p c -> p a c"))
        tab = [sb("tab%d" % a, [P, T], I32) for a in range(PASSES)]
        load(tab[0][:], tab_words[0].rearrange("p t i -> p (t i)").bitcast(I32))
        for row, vector in enumerate((bt, gain)):
            load(vectors[row : row + 1, :], vector.unsqueeze(0))
        load(tab[1][:], tab_words[1].rearrange("p t i -> p (t i)").bitcast(I32))
        turned = bank(7)
        for t in range(PACK):
            nc.tensor.transpose(turned[:, P * t : P * (t + 1)], vectors[:, t:H:PACK], identity[:])
        neg_bt = sb("neg_bt", [P, PACK], F32)
        nc.scalar.mul(neg_bt[:], turned[:, 0:HALF:P], -1.0)
        nc.scalar.copy(gain_sb[:], turned[:, 1:HALF:P])

        picked_sc = sb("picked_sc", [P, S], U8)
        nc.vector.tensor_copy(picked_sc[:], tab_sc[:].indirect(offsets[:]))
        sc_rows = sb("sc_rows", [P, SC], U8)
        nc.vector.tensor_copy(
            sc_rows[:, 0:H].rearrange("p (t m) -> p t m", t=PACK), w2_sc[:].rearrange("p (m t) -> p t m", t=PACK)
        )
        nc.vector.tensor_copy(sc_rows[:, H:SC].bitcast(I32), picked_sc[:].bitcast(I32))

        def move_to_planes(a):
            first_row = ROWS_AT + 16 * a
            for r in range(4):
                load_bytes(planes[a][r:P:32, :], sc_rows[first_row + r : first_row + 16 : 4, :])

        w1_rows = w1.rearrange("(a p j) c -> a p j c", a=PASSES, j=PACK)
        w1_raw = [placed("w1_raw0", [P, PACK, H], F32, 0), placed("w1_raw1", [P, PACK, H], F32, RAW1_AT)]
        move_to_planes(0)
        load(w1_raw[0][:, : PACK - 1], w1_rows[0][:, : PACK - 1])
        move_to_planes(1)
        load(w1_raw[0][:, PACK - 1 :], w1_rows[0][:, PACK - 1 :])
        load(w1_raw[1][:], w1_rows[1])
        w4_raw = sb("w4_raw", [P, PACK, N], F32)
        load(w4_raw[:], w4.rearrange("(p j) n -> p j n", j=PACK))
        for q in range(4):
            load_bytes(w3_sc[32 * q + 8 : 32 * q + 16, :], w3_scales[:, 4 * q : 4 * q + 4, :])
        w3_codes = sb("w3_codes", [P, PASSES, N], I32)
        load(w3_codes[:], w3_words.rearrange("a p c i -> p a (c i)").bitcast(I32))

        v = {}

        def gather(a, hf):
            v[a, hf] = sb("v%d%d" % (a, hf), [P, HALF], U32)[:]
            nc.vector.tensor_copy(v[a, hf], tab[a][:].bitcast(U32).indirect(offsets[:, 32 * hf : 32 * (hf + 1)]))

        w2_codes = sb("w2_codes", [P, PASSES, 2 * H], U8)
        nc.scalar.copy(
            w2_codes[:].bitcast(U16).rearrange("p a (t m) -> p a t m", t=PACK),
            w2_raw[:].bitcast(U16).rearrange("p a (m t) -> p a t m", t=PACK),
        )
        for a in range(PASSES):
            for hf in range(2):
                gather(a, hf)

        def first_stage(acc, codes, scales, a, hf, first):
            nc.tensor.matmul_mx(
                out=acc[:], lhsT=codes, lhsT_scale=scales, rhs=v[a, hf].bitcast(FP8X4),
                rhs_scale=planes[a][:, H + HALF * hf : H + HALF * (hf + 1)], start=(a == first), stop=(a != first),
            )

        peer = {}

        def peer_pass(a, hf, t, first):
            if a == first:
                peer[hf, t] = bank(PACK * hf + t)
            codes = w2_codes[:, a, 2 * P * t : 2 * P * (t + 1)].bitcast(FP4X4)
            first_stage(peer[hf, t], codes, planes[a][:, P * t : P * (t + 1)], a, hf, first)

        w1_bf = {}
        w1_q = {}

        def w1_views(a, t0, m0=0, m1=P):
            dst = w1_bf[a, t0][:].rearrange("p (t m j) -> p m j t", t=2, j=PACK)
            src = w1_raw[a][:].rearrange("p j (m t) -> p m j t", t=PACK)
            return dst[:, m0:m1], src[:, m0:m1, :, t0 : t0 + 2]

        def w1_quantize(a, t0, t1):
            width = P * (t1 - t0)
            codes = sb("w1_codes%d%d" % (a, t0), [P, width], U32)
            scales = sb("w1_sc%d%d" % (a, t0), [P, width], U8)
            pair = t0 - t0 % 2
            source = w1_bf[a, pair][:, H * (t0 - pair) : H * (t1 - pair)]
            nc.vector.quantize_mx(out=codes[:].bitcast(FP8X4), scales=scales[:], in_=source)
            for t in range(t0, t1):
                cols = slice(P * (t - t0), P * (t - t0 + 1))
                w1_q[a, t] = (codes[:, cols].bitcast(FP8X4), scales[:, cols])

        th = {}

        def tanh(hf, t, out):
            th[hf, t] = out
            nc.scalar.activation(out[:], peer[hf, t][:], TANH, bias=neg_bt[:, t : t + 1], scale=-1.0)

        h = {}
        h_rows = out_1.rearrange("(p t) j -> p t j", t=PACK)

        def unexplained(b, hf, t, first):
            act = bank(b)
            for a in (first, 1 - first):
                first_stage(act, w1_q[a, t][0], w1_q[a, t][1], a, hf, first)
            cuts = (0, H_SPLIT[hf], HALF) if (hf, t) == (1, PACK - 1) else (0, HALF)
            for c0, c1 in zip(cuts, cuts[1:]):
                nc.vector.scalar_tensor_tensor(
                    h[hf][:, t, c0:c1], th[hf, t][:, c0:c1], gain_sb[:, t : t + 1], act[:, c0:c1], MULT, ADD
                )
            nc.sync.dma_start(out=h_rows[:, t, HALF * hf : HALF * (hf + 1)], in_=h[hf][:, t, :])

        def gpsimd_cast(dst, src):
            nc.gpsimd.tensor_scalar(dst.rearrange("p (c j) -> p c j", j=PACK), src.rearrange("p j c -> p c j"), 1.0, 0.0, MULT, ADD)

        h_bf = {}

        def h_cast(hf):
            split = H_SPLIT[hf]
            h_bf[hf] = sb("h_bf%d" % hf, [P, PACK * HALF], BF16, tag="h_bf")
            nc.scalar.copy(
                h_bf[hf][:, : PACK * split].rearrange("p (c i t) -> p c t i", i=4, t=PACK),
                h[hf][:, :, :split].rearrange("p t (c i) -> p c t i", i=4),
            )
            gpsimd_cast(h_bf[hf][:, PACK * split :], h[hf][:, :, split:])

        h_codes = [sb("h_codes%d" % hf, [P, HALF], U32) for hf in range(2)]
        h_sc = sb("h_sc", [P, S], U8)
        code_rows = out_2[0].rearrange("p m t -> p (m t)").bitcast(I32)

        def h_quantize(hf):
            cols = slice(HALF * hf, HALF * (hf + 1))
            nc.vector.quantize_mx(out=h_codes[hf][:].bitcast(FP8X4), scales=h_sc[:, cols], in_=h_bf[hf][:])
            nc.sync.dma_start(out=code_rows[:, cols], in_=h_codes[hf][:].bitcast(I32))

        direct = {}

        def direct_tile(b, hf, n):
            acc = bank(b)
            cols = slice(P * n, P * (n + 1))
            for a in range(PASSES):
                first_stage(acc, w3_codes[:, a, cols].bitcast(FP8X4), w3_sc[8 + 4 * a :, cols], a, hf, 0)
            direct[hf, n] = sb("direct%d%d" % (hf, n), [P, HALF], F32)
            nc.scalar.copy(direct[hf, n][:], acc[:])

        def ring_tile(b, hf, n):
            acc = bank(b)
            cols = slice(P * n, P * (n + 1))
            nc.tensor.matmul_mx(
                out=acc[:], lhsT=w4_codes[:, cols].bitcast(FP8X4), lhsT_scale=w4_sc[:, cols],
                rhs=h_codes[hf][:].bitcast(FP8X4), rhs_scale=h_sc[:, HALF * hf : HALF * (hf + 1)], start=True, stop=True,
            )
            cuts = (0, HALF - LAST_PIECE, HALF) if (hf, n) == (1, N_TILES - 1) else (0, HALF)
            for c0, c1 in zip(cuts, cuts[1:]):
                y = sb("y%d%d%d" % (hf, n, c0), [P, c1 - c0], F32)
                nc.vector.tensor_tensor(y[:], acc[:, c0:c1], direct[hf, n][:, c0:c1], MULT)
                nc.sync.dma_start(out=out_0[cols, HALF * hf + c0 : HALF * hf + c1], in_=y[:])

        for a in range(PASSES):
            for hf, t in EARLY_PEERS:
                peer_pass(a, hf, t, 0)
        for t in range(2, PACK):
            for a in (1, 0):
                peer_pass(a, 1, t, 1)
        w1_bf[0, 0] = sb("w1_bf0", [P, PACK * H], BF16)
        for t0 in (0, 2):
            w1_bf[1, t0] = sb("w1_bf1%d" % t0, [P, 2 * H], BF16)
        dst0 = w1_bf[0, 0][:].rearrange("p (t m j) -> p m j t", t=PACK, j=PACK)
        src0 = w1_raw[0][:].rearrange("p j (m t) -> p m j t", t=PACK)
        nc.scalar.copy(dst0[:, M_EARLY:], src0[:, M_EARLY:])
        nc.vector.tensor_copy(dst0[:, :M_EARLY], src0[:, :M_EARLY])
        w1_quantize(0, 0, PACK)
        for t in range(2):
            tanh(0, t, placed("th0%d" % t, [P, HALF], F32, t * SLOT))
        nc.scalar.copy(*w1_views(1, 2, M_SPLIT, P))
        nc.vector.tensor_copy(*w1_views(1, 0))
        nc.vector.tensor_copy(*w1_views(1, 2, 0, M_SPLIT))
        w1_quantize(1, 0, 1)
        w1_quantize(1, 1, 2)
        w1_quantize(1, 2, 4)
        for i, (hf, t) in enumerate(((0, 2), (0, 3), (1, 0), (1, 1), (1, 2))):
            tanh(hf, t, placed("th%d%d" % (hf, t), [P, HALF], F32, LATE_AT + i * SLOT))
        tanh(1, 3, sb("th13", [P, HALF], F32, tag="w1_bf10"))
        for hf in range(2):
            h[hf] = sb("h%d" % hf, [P, PACK, HALF], F32)
        w4_bf = sb("w4_bf", [P, PACK * N], BF16, tag="w1_bf12")
        gpsimd_cast(w4_bf[:], w4_raw[:])

        for t in range(PACK):
            unexplained(t, 0, t, min(t, 1))
        h_cast(0)
        for t in range(PACK - 1):
            unexplained(PACK + t, 1, t, 1)
        direct_tile(7, 0, 0)
        direct_tile(0, 0, 1)
        w4_codes = placed("w4_codes", [P, N], U32, LATE_AT + 3 * SLOT)
        w4_sc = sb("w4_sc", [P, N], U8)
        nc.vector.quantize_mx(out=w4_codes[:].bitcast(FP8X4), scales=w4_sc[:], in_=w4_bf[:])
        h_quantize(0)
        unexplained(6, 1, 3, 1)
        h_cast(1)
        ring_tile(7, 0, 0)
        ring_tile(0, 0, 1)
        direct_tile(1, 0, 2)
        h_quantize(1)
        for r in range(4):
            nc.sync.dma_start(out=out_3[0][r:16:4, :].bitcast(I32), in_=h_sc[r:P:32, :].bitcast(I32))
        ring_tile(4, 0, 2)
        direct_tile(5, 1, 0)
        direct_tile(2, 1, 1)
        ring_tile(3, 1, 0)
        direct_tile(6, 1, 2)
        ring_tile(1, 1, 1)
        ring_tile(7, 1, 2)
